import numpy as np
import ml_dtypes


def mxq(x, axis, fmt="e4m3"):
    dtype, down = {"e4m3": (ml_dtypes.float8_e4m3fn, 7), "e5m2": (ml_dtypes.float8_e5m2, 14)}[fmt]
    v = np.moveaxis(np.asarray(x, np.float32).astype(ml_dtypes.bfloat16).astype(np.float64), axis, -1)
    blocks = v.reshape(v.shape[:-1] + (-1, 32))
    amax = np.abs(blocks).max(-1, keepdims=True)
    byte = np.maximum(np.where(amax > 0, np.frexp(amax)[1] - 1 + 127, 0) - down, 1)
    scale = np.exp2(byte - 127.0)
    codes = (blocks / scale).astype(np.float32).astype(dtype).astype(np.float64)
    return np.moveaxis((codes * scale).reshape(v.shape), -1, axis)


WIDE = False


def mx_kscale(k):
    if not WIDE:
        return np.ones(k)
    levels = np.array([10, -10, 5, -5, 0])
    if k % 512:
        return np.exp2(np.random.permutation(np.resize(levels, k // 32))).repeat(32)
    a = np.empty((k // 512, 16))
    for p in range(k // 512):
        a[p, :8] = np.random.permutation(np.resize(levels, 8))
        for g in range(8):
            far = levels[np.abs(levels - a[p, g]) >= 10]
            a[p, g + 8] = far[np.random.randint(len(far))]
    return np.exp2(a.ravel()).repeat(32)


BF16 = ml_dtypes.bfloat16


def bf(x):
    return np.asarray(x, np.float32).astype(BF16)


def f64(x):
    return np.asarray(x).astype(np.float64)


T, B, R, N = 1024, 1024, 512, 2048

NARROW, BROAD = 0.1, 0.3
SPREAD, MEAN = 4.0, 1.5


def draw0():
    s = mx_kscale(R)
    t = mx_kscale(B)
    phase = np.random.uniform(0.0, 1.0, (T, 1))
    centre = np.random.uniform(0.0, 1.0, (1, B))
    width = np.random.uniform(NARROW, BROAD, (1, B))
    g = np.exp(-0.5 * ((phase - centre) / width) ** 2) / np.sqrt(B)
    factor = SPREAD * np.random.standard_normal((B, R)) / np.sqrt(R)
    noise = np.random.standard_normal((R, N))
    mean = MEAN * np.random.standard_normal(B)
    return {"factor": bf(factor * s * t[:, None]),
            "noise": bf(noise / s[:, None]),
            "mean": bf(mean * t),
            "basis": bf(g / t),
            "rnorm": bf(1.0 / g.sum(axis=1)),
            "amp": bf(1.0 + 0.1 * np.random.standard_normal(N))}


def core(factor, noise, mean, basis, rnorm, amp):
    dev = mxq(f64(factor), 1, "e4m3") @ mxq(f64(noise), 0, "e4m3")
    w = dev + f64(mean)[:, None]
    y = mxq(f64(basis), 1, "e4m3") @ mxq(w, 0, "e4m3")
    return y * f64(rnorm)[:, None] * f64(amp)


def e4m3fn_bytes(y):
    return np.clip(np.asarray(y, np.float64), -448.0, 448.0).astype(np.float32).astype(ml_dtypes.float8_e4m3fn).view(np.uint8)


def e4m3fn_values(b):
    return np.asarray(b, np.uint8).view(ml_dtypes.float8_e4m3fn).astype(np.float64)


def setup_inputs():
    d = draw0()
    x0 = np.asarray(d['noise']).astype(np.float64)
    s = (np.max(np.abs(x0), axis=(1,), keepdims=True) / 448.0).astype(np.float32)
    out = {}
    for k, v in d.items():
        if k == 'noise':
            out['noise_bytes'] = e4m3fn_bytes(x0 / s.astype(np.float64))
            out['noise_scale'] = s
        else:
            out[k] = v
    return out


def reference(factor, noise_bytes, noise_scale, mean, basis, rnorm, amp):
    return core(factor, e4m3fn_values(noise_bytes) * noise_scale.astype(np.float64), mean, basis, rnorm, amp)

@@ -1,0 +1,370 @@
+from contextlib import ExitStack
+
+import concourse.mybir as mybir
+from concourse.masks import make_identity
+
+T, B, R, N = 1024, 1024, 512, 2048
+FLOPS = 2 * B * R * N + 2 * T * B * N
+
+F32 = mybir.dt.float32
+BF16 = mybir.dt.bfloat16
+U32 = mybir.dt.uint32
+U8 = mybir.dt.uint8
+FP8 = mybir.dt.float8_e4m3fn
+FP8X4 = mybir.dt.float8_e4m3fn_x4
+ADD = mybir.AluOpType.add
+MULT = mybir.AluOpType.mult
+COPY = mybir.ActivationFunctionType.Copy
+IDENTITY = mybir.ActivationFunctionType.Identity
+
+P = 128
+PACK = 4
+PASSES = B // (P * PACK)
+CHUNK = 512
+HALF = CHUNK // 2
+CHUNKS = N // CHUNK
+TILES = T // P
+LAST = CHUNKS * TILES - 1
+
+FIRST_ISSUED = (5, 6, 7, 9, 10, 11, 13, 14, 15, 16, 16, 16, 16, 16, 16, 19, 23, 24)
+
+
+def tile_promp_trajectory_sampling_s7_kernel(
+    tc, factor, noise_bytes, noise_scale, mean, basis, rnorm, amp, out
+):
+    nc = tc.nc
+    with ExitStack() as ctx:
+        keep = ctx.enter_context(tc.tile_pool(name="keep", bufs=1))
+        stage = ctx.enter_context(tc.tile_pool(name="stage", bufs=3))
+        psum_first = ctx.enter_context(tc.psum_pool(name="psum_first", bufs=4))
+        psum_second = ctx.enter_context(tc.psum_pool(name="psum_second", bufs=4))
+
+        factor_rows = keep.tile([P, PASSES, PACK, R], BF16, name="factor_rows")
+        factor_woven = keep.tile([P, PASSES, PACK, P, PACK], BF16, name="factor_woven", align_bytes=64)
+        factor_codes = keep.tile([P, PASSES, PACK * P], U32, name="factor_codes", align_bytes=64)
+        factor_scales = keep.tile([P, PASSES, PACK * P], U8, name="factor_scales", align_bytes=64)
+        basis_rows = keep.tile([P, TILES, B], BF16, name="basis_rows")
+        basis_woven = keep.tile([P, TILES, PASSES, P, PACK], BF16, name="basis_woven", align_bytes=64)
+        basis_codes = keep.tile([P, TILES, PASSES * P], U32, name="basis_codes", align_bytes=64)
+        basis_scales = keep.tile([P, TILES, PASSES * P], U8, name="basis_scales", align_bytes=64)
+        noise_codes_in = keep.tile([P, CHUNKS, PACK, CHUNK], U8, name="noise_codes_in")
+        noise_codes = keep.tile([P, CHUNKS, CHUNK], U32, name="noise_codes", align_bytes=64)
+        noise_scales = keep.tile([P, CHUNKS, CHUNK], U8, name="noise_scales", align_bytes=64)
+        byte_scale = keep.tile([P, PACK], F32, name="byte_scale")
+        mean_in = keep.tile([P, PASSES, PACK], BF16, name="mean_in")
+        mean_f32 = keep.tile([P, PASSES, PACK], F32, name="mean_f32")
+        rnorm_in = keep.tile([P, TILES], BF16, name="rnorm_in")
+        rnorm_f32 = keep.tile([P, TILES], F32, name="rnorm_f32")
+        amp_all = keep.tile([P, N], BF16, name="amp_all")
+        identity = keep.tile([P, P], F32, name="identity")
+        warm = keep.tile([P, 1], F32, name="warm")
+
+        factor_hbm = factor.rearrange("(g m t) r -> g m t r", g=PASSES, t=PACK)
+        noise_hbm = noise_bytes.rearrange("(p t) (c j) -> c p t j", t=PACK, j=CHUNK)
+        basis_hbm = basis.rearrange("(p n) b -> p n b", n=TILES)
+        out_hbm = out.rearrange("(p n) j -> p n j", n=TILES)
+
+        def load_factor(g, a):
+            slots = slice(2 * a, 2 * a + 2)
+            nc.sync.dma_start(out=factor_rows[:, g, slots, :], in_=factor_hbm[g][:, slots, :])
+
+        def load_noise(c):
+            nc.sync.dma_start(out=noise_codes_in[:, c], in_=noise_hbm[c])
+
+        def load_basis(n):
+            nc.sync.dma_start(out=basis_rows[:, n : n + 2, :], in_=basis_hbm[:, n : n + 2, :])
+
+        def load_amp(first, end):
+            cols = slice(CHUNK * first, CHUNK * end)
+            nc.sync.dma_start(out=amp_all[:, cols], in_=amp[cols].partition_broadcast(P))
+
+        nc.sync.dma_start(out=byte_scale[:], in_=noise_scale.rearrange("(p t) o -> p (t o)", t=PACK))
+        nc.scalar.dma_start(out=mean_in[:], in_=mean.rearrange("(g p t) -> p g t", g=PASSES, t=PACK))
+        nc.scalar.dma_start(out=rnorm_in[:], in_=rnorm.rearrange("(p n) -> p n", n=TILES))
+        for t in (0, 2):
+            nc.sync.dma_start(out=noise_codes_in[:, 0, t : t + 2], in_=noise_hbm[0][:, t : t + 2])
+        for g in range(PASSES):
+            for a in range(2):
+                load_factor(g, a)
+        load_basis(0)
+        load_noise(1)
+        load_basis(2)
+        load_noise(2)
+        load_basis(4)
+        load_amp(0, 1)
+        load_basis(6)
+        load_noise(3)
+        load_amp(1, CHUNKS)
+
+        make_identity(nc, identity[:])
+        nc.vector.memset(warm[:], 0.0)
+        nc.scalar.activation(out=warm[:], in_=warm[:], func=IDENTITY)
+
+        factor_words = factor_rows[:].bitcast(F32)
+        basis_words = basis_rows[:].bitcast(F32)
+
+        def turn_factor(g, a):
+            bank = psum_first.tile([P, 2, 2, P], F32, name="bank_first")
+            for x in range(2):
+                for u in range(2):
+                    nc.tensor.transpose(bank[:, x, u, :], factor_words[:, g, 2 * a + x, u::2], identity[:])
+            return bank
+
+        def empty_factor(copy, bank, g, a):
+            woven = factor_woven[:, g, 2 * a : 2 * a + 2].rearrange("p x m t -> p (x m t)").bitcast(F32)
+            copy(
+                out=woven.rearrange("p (x m u) -> p x m u", x=2, u=2),
+                in_=bank[:].rearrange("p x u m -> p x m u"),
+            )
+
+        def quantize_factor(g):
+            nc.vector.quantize_mx(
+                out=factor_codes[:, g].bitcast(FP8X4),
+                scales=factor_scales[:, g],
+                in_=factor_woven[:, g].rearrange("p t m k -> p (t m k)"),
+            )
+
+        def turn_basis(n):
+            bank = psum_second.tile([P, PASSES, 2, P], F32, name="bank_second")
+            for g in range(PASSES):
+                first = P * 2 * g
+                for u in range(2):
+                    words = slice(first + u, first + P * 2, 2)
+                    nc.tensor.transpose(bank[:, g, u, :], basis_words[:, n, words], identity[:])
+            return bank
+
+        def empty_basis(bank, n):
+            woven = basis_woven[:, n].rearrange("p g m t -> p (g m t)").bitcast(F32)
+            nc.scalar.copy(
+                out=woven.rearrange("p (g m u) -> p g m u", g=PASSES, u=2),
+                in_=bank[:].rearrange("p g u m -> p g m u"),
+            )
+
+        def quantize_basis(n):
+            pair = slice(n, n + 2)
+            nc.vector.quantize_mx(
+                out=basis_codes[:, pair].rearrange("p n k -> p (n k)").bitcast(FP8X4),
+                scales=basis_scales[:, pair].rearrange("p n k -> p (n k)"),
+                in_=basis_woven[:, pair].rearrange("p n g m t -> p (n g m t)"),
+            )
+
+        def weave(engine, woven, planes, half):
+            cols = slice(HALF * half, HALF * (half + 1))
+            dst = woven[:, cols, :]
+            src = planes[:, :, cols]
+            if engine == "gpsimd":
+                nc.gpsimd.tensor_scalar(
+                    out=dst, in0=src.rearrange("p t j -> p j t"), scalar1=1.0, scalar2=0.0, op0=MULT, op1=ADD
+                )
+                return
+            copy = nc.scalar.copy if engine == "scalar" else nc.vector.tensor_copy
+            copy(
+                out=dst.rearrange("p (j i) t -> p j t i", i=4),
+                in_=src.rearrange("p t (j i) -> p j t i", i=4),
+            )
+
+        noise_planes = {}
+        noise_woven = {}
+
+        def widen_noise(engine, c):
+            noise_planes[c] = stage.tile([P, PACK, CHUNK], BF16, name="noise_planes")
+            noise_woven[c] = stage.tile([P, CHUNK, PACK], BF16, name="noise_woven", align_bytes=64)
+            for t in range(PACK):
+                src = noise_codes_in[:, c, t, :].bitcast(FP8)
+                dst = noise_planes[c][:, t, :]
+                scale = byte_scale[:, t : t + 1]
+                if engine == "scalar":
+                    nc.scalar.activation(out=dst, in_=src, func=COPY, scale=scale)
+                else:
+                    nc.vector.tensor_scalar(out=dst, in0=src, scalar1=scale, scalar2=None, op0=MULT)
+
+        def weave_noise(engine, c, half):
+            weave(engine, noise_woven[c], noise_planes[c], half)
+
+        def quantize_noise(c):
+            nc.vector.quantize_mx(
+                out=noise_codes[:, c].bitcast(FP8X4),
+                scales=noise_scales[:, c],
+                in_=noise_woven[c][:].rearrange("p j t -> p (j t)"),
+            )
+
+        w_planes = {}
+        w_woven = {}
+        w_codes = {}
+        w_scales = {}
+
+        def first_pass(bank, g, t, c, cols):
+            rows = slice(P * t, P * (t + 1))
+            nc.tensor.matmul_mx(
+                out=bank,
+                lhsT=factor_codes[:, g, rows].bitcast(FP8X4),
+                lhsT_scale=factor_scales[:, g, rows],
+                rhs=noise_codes[:, c, cols].bitcast(FP8X4),
+                rhs_scale=noise_scales[:, c, cols],
+                start=True,
+                stop=True,
+            )
+
+        def w_tiles(c, g):
+            w_woven[c, g] = stage.tile([P, CHUNK, PACK], BF16, name="w_woven", align_bytes=64, bufs=4)
+            w_codes[c, g] = stage.tile([P, CHUNK], U32, name="w_codes", align_bytes=64, bufs=6)
+            w_scales[c, g] = stage.tile([P, CHUNK], U8, name="w_scales", align_bytes=64, bufs=6)
+
+        def first_woven(g, quarter):
+            bank = psum_first.tile([P, PACK, P], F32, name="bank_first")
+            cols = slice(P * quarter, P * (quarter + 1))
+            for t in range(PACK):
+                first_pass(bank[:, t, :], g, t, 0, cols)
+            return bank
+
+        def empty_woven(bank, g, quarter):
+            nc.vector.tensor_tensor(
+                out=w_woven[0, g][:, P * quarter : P * (quarter + 1), :],
+                in0=bank[:].rearrange("p t j -> p j t"),
+                in1=mean_f32[:, g, :].unsqueeze(1).to_broadcast([P, P, PACK]),
+                op=ADD,
+            )
+
+        def first_plane(c, g, t):
+            if t == 0:
+                w_tiles(c, g)
+                w_planes[c, g] = stage.tile([P, PACK, CHUNK], BF16, name="w_planes", bufs=4)
+            bank = psum_first.tile([P, CHUNK], F32, name="bank_first")
+            first_pass(bank[:], g, t, c, slice(0, CHUNK))
+            nc.scalar.activation(
+                out=w_planes[c, g][:, t, :], in_=bank[:], func=IDENTITY, bias=mean_f32[:, g, t : t + 1]
+            )
+
+        def weave_w(engine, c, g, half):
+            weave(engine, w_woven[c, g], w_planes[c, g], half)
+
+        def quantize_w(c, g, cols):
+            nc.vector.quantize_mx(
+                out=w_codes[c, g][:, cols].bitcast(FP8X4),
+                scales=w_scales[c, g][:, cols],
+                in_=w_woven[c, g][:, cols, :].rearrange("p j t -> p (j t)"),
+            )
+
+        whole = slice(0, CHUNK)
+        halves = (slice(0, HALF), slice(HALF, CHUNK))
+
+        results = {}
+
+        def second_tile(s):
+            c, n = divmod(s, TILES)
+            bank = psum_second.tile([P, CHUNK], F32, name="bank_second")
+            for g in range(PASSES):
+                phases = slice(P * g, P * (g + 1))
+                nc.tensor.matmul_mx(
+                    out=bank[:],
+                    lhsT=basis_codes[:, n, phases].bitcast(FP8X4),
+                    lhsT_scale=basis_scales[:, n, phases],
+                    rhs=w_codes[c, g][:].bitcast(FP8X4),
+                    rhs_scale=w_scales[c, g][:],
+                    start=(g == 0),
+                    stop=(g == PASSES - 1),
+                )
+            return bank
+
+        def finish_tile(s, bank):
+            c, n = divmod(s, TILES)
+            if n % 2 == 0:
+                results[s // 2] = stage.tile([P, 2, CHUNK], F32, name="result", bufs=5)
+            result = results[s // 2]
+            for cols in halves if s == LAST else (whole,):
+                out_cols = slice(CHUNK * c + cols.start, CHUNK * c + cols.stop)
+                nc.vector.scalar_tensor_tensor(
+                    out=result[:, n % 2, cols],
+                    in0=bank[:, cols],
+                    scalar=rnorm_f32[:, n : n + 1],
+                    in1=amp_all[:, out_cols],
+                    op0=MULT,
+                    op1=MULT,
+                )
+                if s >= LAST - 1:
+                    nc.sync.dma_start(out=out_hbm[:, n, out_cols], in_=result[:, n % 2, cols])
+            if n % 2 == 1 and s != LAST:
+                nc.sync.dma_start(out=out_hbm[:, n - 1 : n + 1, CHUNK * c : CHUNK * (c + 1)], in_=result[:])
+
+        with tc.manual_schedule():
+            nc.vector.tensor_copy(out=mean_f32[:], in_=mean_in[:])
+            nc.vector.tensor_copy(out=rnorm_f32[:], in_=rnorm_in[:])
+
+            widen_noise("vector", 0)
+            weave_noise("vector", 0, 0)
+            weave_noise("vector", 0, 1)
+            quantize_noise(0)
+            turned = {}
+            for g in range(PASSES):
+                for a in range(2):
+                    turned[g, a] = turn_factor(g, a)
+            empty_factor(nc.scalar.copy, turned[0, 0], 0, 0)
+            empty_factor(nc.scalar.copy, turned[0, 1], 0, 1)
+            quantize_factor(0)
+            empty_factor(nc.scalar.copy, turned[1, 0], 1, 0)
+            empty_factor(nc.vector.tensor_copy, turned[1, 1], 1, 1)
+            quantize_factor(1)
+
+            basis_bank = {}
+            for g in range(PASSES):
+                w_tiles(0, g)
+                for quarter in range(4):
+                    empty_woven(first_woven(g, quarter), g, quarter)
+                if g == 0:
+                    for n in range(2):
+                        basis_bank[n] = turn_basis(n)
+            for g in range(PASSES):
+                quantize_w(0, g, whole)
+
+            widen_noise("scalar", 1)
+            weave_noise("gpsimd", 1, 0)
+            weave_noise("gpsimd", 1, 1)
+            quantize_noise(1)
+            widen_noise("scalar", 2)
+            weave_noise("gpsimd", 2, 0)
+            weave_noise("vector", 2, 1)
+
+            for n in range(TILES):
+                if n >= 2:
+                    basis_bank[n] = turn_basis(n)
+                empty_basis(basis_bank[n], n)
+                if n % 2 == 1:
+                    quantize_basis(n - 1)
+            quantize_noise(2)
+
+            issued = 0
+            for s in range(CHUNKS * TILES):
+                if s == 5:
+                    widen_noise("scalar", 3)
+                while issued < FIRST_ISSUED[min(s, len(FIRST_ISSUED) - 1)]:
+                    c, bank_of_chunk = divmod(issued, PASSES * PACK)
+                    g, t = divmod(bank_of_chunk, PACK)
+                    first_plane(c + 1, g, t)
+                    issued += 1
+
+                if s == 0:
+                    for half in range(2):
+                        weave_w("vector", 1, 0, half)
+                    for half in range(2):
+                        quantize_w(1, 0, halves[half])
+                if s == 3:
+                    weave_w("gpsimd", 1, 1, 0)
+                    weave_w("vector", 1, 1, 1)
+                    for half in range(2):
+                        quantize_w(1, 1, halves[half])
+                if s == 11:
+                    for half in range(2):
+                        weave_noise("gpsimd", 3, half)
+                    quantize_noise(3)
+                if s == 14:
+                    for engine, g in (("scalar", 1), ("gpsimd", 0)):
+                        weave_w(engine, 2, g, 1)
+                        weave_w(engine, 2, g, 0)
+                        quantize_w(2, g, whole)
+                if s == 22:
+                    for g, engines in enumerate((("gpsimd", "scalar"), ("scalar", "gpsimd"))):
+                        for half in range(2):
+                            weave_w(engines[half], 3, g, half)
+                        quantize_w(3, g, whole)
+
+                finish_tile(s, second_tile(s))

@@ -20,13 +20,27 @@ IDENTITY = mybir.ActivationFunctionType.Identity
 P = 128
 PACK = 4
 PASSES = B // (P * PACK)
-CHUNK = 512
-HALF = CHUNK // 2
-CHUNKS = N // CHUNK
+BANK = 512
+HALF = BANK // 2
 TILES = T // P
-LAST = CHUNKS * TILES - 1
+WIDTHS = (HALF, BANK, BANK, BANK, HALF)
+STARTS = tuple(sum(WIDTHS[:c]) for c in range(len(WIDTHS)))
+CHUNKS = len(WIDTHS)
 
-FIRST_ISSUED = (5, 6, 7, 9, 10, 11, 13, 14, 15, 16, 16, 16, 16, 16, 16, 19, 23, 24)
+
+def piece_of(c, g):
+    if c == 0:
+        return 0, HALF * g
+    if c == CHUNKS - 1:
+        return 2 * c - 1, HALF * g
+    return 2 * c - 1 + g, 0
+
+
+def source_of(u, col):
+    c = (u + 1) // 2
+    if WIDTHS[c] == HALF:
+        return col // HALF, STARTS[c] + col % HALF
+    return (u - 1) % 2, STARTS[c] + col
 
 
 def tile_promp_trajectory_sampling_s7_kernel(
@@ -35,83 +49,70 @@ def tile_promp_trajectory_sampling_s7_kernel(
     nc = tc.nc
     with ExitStack() as ctx:
         keep = ctx.enter_context(tc.tile_pool(name="keep", bufs=1))
-        stage = ctx.enter_context(tc.tile_pool(name="stage", bufs=3))
-        psum_first = ctx.enter_context(tc.psum_pool(name="psum_first", bufs=4))
-        psum_second = ctx.enter_context(tc.psum_pool(name="psum_second", bufs=4))
+        stage = ctx.enter_context(tc.tile_pool(name="stage", bufs=2))
+        psum_a = ctx.enter_context(tc.psum_pool(name="psum_a", bufs=8))
+        psum_b = psum_a
 
-        factor_rows = keep.tile([P, PASSES, PACK, R], BF16, name="factor_rows")
-        factor_woven = keep.tile([P, PASSES, PACK, P, PACK], BF16, name="factor_woven", align_bytes=64)
+        factor_woven = {}
         factor_codes = keep.tile([P, PASSES, PACK * P], U32, name="factor_codes", align_bytes=64)
         factor_scales = keep.tile([P, PASSES, PACK * P], U8, name="factor_scales", align_bytes=64)
-        basis_rows = keep.tile([P, TILES, B], BF16, name="basis_rows")
         basis_woven = keep.tile([P, TILES, PASSES, P, PACK], BF16, name="basis_woven", align_bytes=64)
         basis_codes = keep.tile([P, TILES, PASSES * P], U32, name="basis_codes", align_bytes=64)
         basis_scales = keep.tile([P, TILES, PASSES * P], U8, name="basis_scales", align_bytes=64)
-        noise_codes_in = keep.tile([P, CHUNKS, PACK, CHUNK], U8, name="noise_codes_in")
-        noise_codes = keep.tile([P, CHUNKS, CHUNK], U32, name="noise_codes", align_bytes=64)
-        noise_scales = keep.tile([P, CHUNKS, CHUNK], U8, name="noise_scales", align_bytes=64)
+        noise_codes = keep.tile([P, N], U32, name="noise_codes", align_bytes=64)
+        noise_scales = keep.tile([P, N], U8, name="noise_scales", align_bytes=64)
         byte_scale = keep.tile([P, PACK], F32, name="byte_scale")
-        mean_in = keep.tile([P, PASSES, PACK], BF16, name="mean_in")
-        mean_f32 = keep.tile([P, PASSES, PACK], F32, name="mean_f32")
-        rnorm_in = keep.tile([P, TILES], BF16, name="rnorm_in")
-        rnorm_f32 = keep.tile([P, TILES], F32, name="rnorm_f32")
-        amp_all = keep.tile([P, N], BF16, name="amp_all")
+        mean_cols = keep.tile([P, PASSES, PACK], BF16, name="mean_cols")
+        rnorm_cols = keep.tile([P, TILES], BF16, name="rnorm_cols")
         identity = keep.tile([P, P], F32, name="identity")
-        warm = keep.tile([P, 1], F32, name="warm")
 
         factor_hbm = factor.rearrange("(g m t) r -> g m t r", g=PASSES, t=PACK)
-        noise_hbm = noise_bytes.rearrange("(p t) (c j) -> c p t j", t=PACK, j=CHUNK)
+        noise_hbm = noise_bytes.rearrange("(p t) j -> p t j", t=PACK)
         basis_hbm = basis.rearrange("(p n) b -> p n b", n=TILES)
         out_hbm = out.rearrange("(p n) j -> p n j", n=TILES)
 
+        factor_rows = {}
+        basis_rows = {}
+        noise_in = {}
+        amp_rows = {}
+
+        def columns(c):
+            return slice(STARTS[c], STARTS[c] + WIDTHS[c])
+
         def load_factor(g, a):
-            slots = slice(2 * a, 2 * a + 2)
-            nc.sync.dma_start(out=factor_rows[:, g, slots, :], in_=factor_hbm[g][:, slots, :])
+            factor_rows[g, a] = keep.tile([P, 2, R], BF16, name=f"factor_rows_{g}_{a}")
+            nc.sync.dma_start(out=factor_rows[g, a][:], in_=factor_hbm[g][:, 2 * a : 2 * a + 2, :])
 
-        def load_noise(c):
-            nc.sync.dma_start(out=noise_codes_in[:, c], in_=noise_hbm[c])
+        def load_noise(first, end):
+            lo, hi = STARTS[first], STARTS[end - 1] + WIDTHS[end - 1]
+            bytes_in = keep.tile([P, PACK, hi - lo], U8, name=f"noise_in_{first}")
+            nc.sync.dma_start(out=bytes_in[:], in_=noise_hbm[:, :, lo:hi])
+            for c in range(first, end):
+                noise_in[c] = bytes_in[:, :, STARTS[c] - lo : STARTS[c] - lo + WIDTHS[c]]
 
-        def load_basis(n):
-            nc.sync.dma_start(out=basis_rows[:, n : n + 2, :], in_=basis_hbm[:, n : n + 2, :])
+        def load_basis(first, end):
+            rows = keep.tile([P, end - first, B], BF16, name=f"basis_rows_{first}")
+            nc.sync.dma_start(out=rows[:], in_=basis_hbm[:, first:end, :])
+            for n in range(first, end):
+                basis_rows[n] = rows[:, n - first, :]
 
         def load_amp(first, end):
-            cols = slice(CHUNK * first, CHUNK * end)
-            nc.sync.dma_start(out=amp_all[:, cols], in_=amp[cols].partition_broadcast(P))
+            lo, hi = STARTS[first], STARTS[end - 1] + WIDTHS[end - 1]
+            rows = keep.tile([P, hi - lo], BF16, name=f"amp_rows_{first}")
+            nc.sync.dma_start(out=rows[:], in_=amp[lo:hi].partition_broadcast(P))
+            for c in range(first, end):
+                amp_rows[c] = rows[:, STARTS[c] - lo : STARTS[c] - lo + WIDTHS[c]]
 
-        nc.sync.dma_start(out=byte_scale[:], in_=noise_scale.rearrange("(p t) o -> p (t o)", t=PACK))
-        nc.scalar.dma_start(out=mean_in[:], in_=mean.rearrange("(g p t) -> p g t", g=PASSES, t=PACK))
-        nc.scalar.dma_start(out=rnorm_in[:], in_=rnorm.rearrange("(p n) -> p n", n=TILES))
-        for t in (0, 2):
-            nc.sync.dma_start(out=noise_codes_in[:, 0, t : t + 2], in_=noise_hbm[0][:, t : t + 2])
-        for g in range(PASSES):
-            for a in range(2):
-                load_factor(g, a)
-        load_basis(0)
-        load_noise(1)
-        load_basis(2)
-        load_noise(2)
-        load_basis(4)
-        load_amp(0, 1)
-        load_basis(6)
-        load_noise(3)
-        load_amp(1, CHUNKS)
-
-        make_identity(nc, identity[:])
-        nc.vector.memset(warm[:], 0.0)
-        nc.scalar.activation(out=warm[:], in_=warm[:], func=IDENTITY)
-
-        factor_words = factor_rows[:].bitcast(F32)
-        basis_words = basis_rows[:].bitcast(F32)
-
-        def turn_factor(g, a):
-            bank = psum_first.tile([P, 2, 2, P], F32, name="bank_first")
+        def turn_factor(pool, g, a):
+            bank = pool.tile([P, 2, 2, P], F32, name="bank")
+            words = factor_rows[g, a][:].bitcast(F32)
             for x in range(2):
                 for u in range(2):
-                    nc.tensor.transpose(bank[:, x, u, :], factor_words[:, g, 2 * a + x, u::2], identity[:])
+                    nc.tensor.transpose(bank[:, x, u, :], words[:, x, u::2], identity[:])
             return bank
 
         def empty_factor(copy, bank, g, a):
-            woven = factor_woven[:, g, 2 * a : 2 * a + 2].rearrange("p x m t -> p (x m t)").bitcast(F32)
+            woven = factor_woven[g][:, HALF * a : HALF * (a + 1), :].rearrange("p m t -> p (m t)").bitcast(F32)
             copy(
                 out=woven.rearrange("p (x m u) -> p x m u", x=2, u=2),
                 in_=bank[:].rearrange("p x u m -> p x m u"),
@@ -121,37 +122,36 @@ def tile_promp_trajectory_sampling_s7_kernel(
             nc.vector.quantize_mx(
                 out=factor_codes[:, g].bitcast(FP8X4),
                 scales=factor_scales[:, g],
-                in_=factor_woven[:, g].rearrange("p t m k -> p (t m k)"),
+                in_=factor_woven[g][:].rearrange("p m t -> p (m t)"),
             )
 
-        def turn_basis(n):
-            bank = psum_second.tile([P, PASSES, 2, P], F32, name="bank_second")
+        def turn_basis(pool, n):
+            bank = pool.tile([P, PASSES, 2, P], F32, name="bank")
+            words = basis_rows[n].bitcast(F32)
             for g in range(PASSES):
                 first = P * 2 * g
                 for u in range(2):
-                    words = slice(first + u, first + P * 2, 2)
-                    nc.tensor.transpose(bank[:, g, u, :], basis_words[:, n, words], identity[:])
+                    nc.tensor.transpose(bank[:, g, u, :], words[:, first + u : first + P * 2 : 2], identity[:])
             return bank
 
-        def empty_basis(bank, n):
+        def empty_basis(copy, bank, n):
             woven = basis_woven[:, n].rearrange("p g m t -> p (g m t)").bitcast(F32)
-            nc.scalar.copy(
+            copy(
                 out=woven.rearrange("p (g m u) -> p g m u", g=PASSES, u=2),
                 in_=bank[:].rearrange("p g u m -> p g m u"),
             )
 
-        def quantize_basis(n):
-            pair = slice(n, n + 2)
+        def quantize_basis(first, end):
+            some = slice(first, end)
             nc.vector.quantize_mx(
-                out=basis_codes[:, pair].rearrange("p n k -> p (n k)").bitcast(FP8X4),
-                scales=basis_scales[:, pair].rearrange("p n k -> p (n k)"),
-                in_=basis_woven[:, pair].rearrange("p n g m t -> p (n g m t)"),
+                out=basis_codes[:, some].rearrange("p n k -> p (n k)").bitcast(FP8X4),
+                scales=basis_scales[:, some].rearrange("p n k -> p (n k)"),
+                in_=basis_woven[:, some].rearrange("p n g m t -> p (n g m t)"),
             )
 
-        def weave(engine, woven, planes, half):
-            cols = slice(HALF * half, HALF * (half + 1))
-            dst = woven[:, cols, :]
-            src = planes[:, :, cols]
+        def weave(engine, woven, planes, first, end):
+            dst = woven[:, first:end, :]
+            src = planes[:, :, first:end]
             if engine == "gpsimd":
                 nc.gpsimd.tensor_scalar(
                     out=dst, in0=src.rearrange("p t j -> p j t"), scalar1=1.0, scalar2=0.0, op0=MULT, op1=ADD
@@ -166,11 +166,11 @@ def tile_promp_trajectory_sampling_s7_kernel(
         noise_planes = {}
         noise_woven = {}
 
-        def widen_noise(engine, c):
-            noise_planes[c] = stage.tile([P, PACK, CHUNK], BF16, name="noise_planes")
-            noise_woven[c] = stage.tile([P, CHUNK, PACK], BF16, name="noise_woven", align_bytes=64)
-            for t in range(PACK):
-                src = noise_codes_in[:, c, t, :].bitcast(FP8)
+        def widen_noise(engine, c, first=0, end=PACK):
+            if c not in noise_planes:
+                noise_planes[c] = stage.tile([P, PACK, WIDTHS[c]], BF16, name="noise_planes", bufs=4)
+            for t in range(first, end):
+                src = noise_in[c][:, t, :].bitcast(FP8)
                 dst = noise_planes[c][:, t, :]
                 scale = byte_scale[:, t : t + 1]
                 if engine == "scalar":
@@ -178,14 +178,17 @@ def tile_promp_trajectory_sampling_s7_kernel(
                 else:
                     nc.vector.tensor_scalar(out=dst, in0=src, scalar1=scale, scalar2=None, op0=MULT)
 
-        def weave_noise(engine, c, half):
-            weave(engine, noise_woven[c], noise_planes[c], half)
+        def woven_tile(tag, bufs):
+            return stage.tile([P, BANK, PACK], BF16, name=tag, align_bytes=64, bufs=bufs)
+
+        def weave_noise(engine, c, first, end):
+            weave(engine, noise_woven[c], noise_planes[c], first, end)
 
         def quantize_noise(c):
             nc.vector.quantize_mx(
-                out=noise_codes[:, c].bitcast(FP8X4),
-                scales=noise_scales[:, c],
-                in_=noise_woven[c][:].rearrange("p j t -> p (j t)"),
+                out=noise_codes[:, columns(c)].bitcast(FP8X4),
+                scales=noise_scales[:, columns(c)],
+                in_=noise_woven[c][:, : WIDTHS[c], :].rearrange("p j t -> p (j t)"),
             )
 
         w_planes = {}
@@ -193,178 +196,225 @@ def tile_promp_trajectory_sampling_s7_kernel(
         w_codes = {}
         w_scales = {}
 
-        def first_pass(bank, g, t, c, cols):
+        def first_pass(dst, g, t, j, width):
             rows = slice(P * t, P * (t + 1))
             nc.tensor.matmul_mx(
-                out=bank,
+                out=dst,
                 lhsT=factor_codes[:, g, rows].bitcast(FP8X4),
                 lhsT_scale=factor_scales[:, g, rows],
-                rhs=noise_codes[:, c, cols].bitcast(FP8X4),
-                rhs_scale=noise_scales[:, c, cols],
+                rhs=noise_codes[:, j : j + width].bitcast(FP8X4),
+                rhs_scale=noise_scales[:, j : j + width],
                 start=True,
                 stop=True,
             )
 
-        def w_tiles(c, g):
-            w_woven[c, g] = stage.tile([P, CHUNK, PACK], BF16, name="w_woven", align_bytes=64, bufs=4)
-            w_codes[c, g] = stage.tile([P, CHUNK], U32, name="w_codes", align_bytes=64, bufs=6)
-            w_scales[c, g] = stage.tile([P, CHUNK], U8, name="w_scales", align_bytes=64, bufs=6)
-
-        def first_woven(g, quarter):
-            bank = psum_first.tile([P, PACK, P], F32, name="bank_first")
-            cols = slice(P * quarter, P * (quarter + 1))
+        def first_quarter(pool, u, quarter):
+            g, j = source_of(u, P * quarter)
+            bank = pool.tile([P, PACK, P], F32, name="bank")
             for t in range(PACK):
-                first_pass(bank[:, t, :], g, t, 0, cols)
+                first_pass(bank[:, t, :], g, t, j, P)
             return bank
 
-        def empty_woven(bank, g, quarter):
+        def empty_quarter(bank, u, quarter):
+            g, j = source_of(u, P * quarter)
             nc.vector.tensor_tensor(
-                out=w_woven[0, g][:, P * quarter : P * (quarter + 1), :],
+                out=w_woven[u][:, P * quarter : P * (quarter + 1), :],
                 in0=bank[:].rearrange("p t j -> p j t"),
-                in1=mean_f32[:, g, :].unsqueeze(1).to_broadcast([P, P, PACK]),
+                in1=mean_cols[:, g, :].unsqueeze(1).to_broadcast([P, P, PACK]),
                 op=ADD,
             )
 
-        def first_plane(c, g, t):
-            if t == 0:
-                w_tiles(c, g)
-                w_planes[c, g] = stage.tile([P, PACK, CHUNK], BF16, name="w_planes", bufs=4)
-            bank = psum_first.tile([P, CHUNK], F32, name="bank_first")
-            first_pass(bank[:], g, t, c, slice(0, CHUNK))
-            nc.scalar.activation(
-                out=w_planes[c, g][:, t, :], in_=bank[:], func=IDENTITY, bias=mean_f32[:, g, t : t + 1]
-            )
+        def first_bank(pool, u, x):
+            if x == 0:
+                w_planes[u] = stage.tile([P, PACK, BANK], BF16, name="w_planes", bufs=3)
+            bank = pool.tile([P, BANK], F32, name="bank")
+            if WIDTHS[(u + 1) // 2] == BANK:
+                g, j = source_of(u, 0)
+                parts = [(g, x, j, 0, 0, BANK)]
+            else:
+                g, j = source_of(u, HALF * (x // 2))
+                parts = [(g, 2 * (x % 2) + y, j, HALF * y, HALF * g, HALF) for y in range(2)]
+            for g, t, j, at, to, width in parts:
+                first_pass(bank[:, at : at + width], g, t, j, width)
+            for g, t, j, at, to, width in parts:
+                nc.scalar.activation(
+                    out=w_planes[u][:, t, to : to + width],
+                    in_=bank[:, at : at + width],
+                    func=IDENTITY,
+                    bias=mean_cols[:, g, t : t + 1],
+                )
 
-        def weave_w(engine, c, g, half):
-            weave(engine, w_woven[c, g], w_planes[c, g], half)
+        def weave_w(engine, u, first, end):
+            weave(engine, w_woven[u], w_planes[u], first, end)
 
-        def quantize_w(c, g, cols):
+        def quantize_w(u):
+            w_codes[u] = keep.tile([P, BANK], U32, name=f"w_codes_{u}", align_bytes=64)
+            w_scales[u] = keep.tile([P, BANK], U8, name=f"w_scales_{u}", align_bytes=64)
             nc.vector.quantize_mx(
-                out=w_codes[c, g][:, cols].bitcast(FP8X4),
-                scales=w_scales[c, g][:, cols],
-                in_=w_woven[c, g][:, cols, :].rearrange("p j t -> p (j t)"),
+                out=w_codes[u][:].bitcast(FP8X4),
+                scales=w_scales[u][:],
+                in_=w_woven[u][:].rearrange("p j t -> p (j t)"),
             )
-
-        whole = slice(0, CHUNK)
-        halves = (slice(0, HALF), slice(HALF, CHUNK))
 
         results = {}
 
-        def second_tile(s):
-            c, n = divmod(s, TILES)
-            bank = psum_second.tile([P, CHUNK], F32, name="bank_second")
+        def second_tile(pool, c, n):
+            bank = pool.tile([P, WIDTHS[c]], F32, name="bank")
             for g in range(PASSES):
+                u, at = piece_of(c, g)
                 phases = slice(P * g, P * (g + 1))
                 nc.tensor.matmul_mx(
                     out=bank[:],
                     lhsT=basis_codes[:, n, phases].bitcast(FP8X4),
                     lhsT_scale=basis_scales[:, n, phases],
-                    rhs=w_codes[c, g][:].bitcast(FP8X4),
-                    rhs_scale=w_scales[c, g][:],
+                    rhs=w_codes[u][:, at : at + WIDTHS[c]].bitcast(FP8X4),
+                    rhs_scale=w_scales[u][:, at : at + WIDTHS[c]],
                     start=(g == 0),
                     stop=(g == PASSES - 1),
                 )
             return bank
 
-        def finish_tile(s, bank):
-            c, n = divmod(s, TILES)
+        def finish_tile(bank, c, n):
             if n % 2 == 0:
-                results[s // 2] = stage.tile([P, 2, CHUNK], F32, name="result", bufs=5)
-            result = results[s // 2]
-            for cols in halves if s == LAST else (whole,):
-                out_cols = slice(CHUNK * c + cols.start, CHUNK * c + cols.stop)
-                nc.vector.scalar_tensor_tensor(
-                    out=result[:, n % 2, cols],
-                    in0=bank[:, cols],
-                    scalar=rnorm_f32[:, n : n + 1],
-                    in1=amp_all[:, out_cols],
-                    op0=MULT,
-                    op1=MULT,
-                )
-                if s >= LAST - 1:
-                    nc.sync.dma_start(out=out_hbm[:, n, out_cols], in_=result[:, n % 2, cols])
-            if n % 2 == 1 and s != LAST:
-                nc.sync.dma_start(out=out_hbm[:, n - 1 : n + 1, CHUNK * c : CHUNK * (c + 1)], in_=result[:])
+                results[c, n // 2] = stage.tile([P, 2, WIDTHS[c]], F32, name="result", bufs=6)
+            result = results[c, n // 2]
+            nc.vector.scalar_tensor_tensor(
+                out=result[:, n % 2, :],
+                in0=bank[:],
+                scalar=rnorm_cols[:, n : n + 1],
+                in1=amp_rows[c],
+                op0=MULT,
+                op1=MULT,
+            )
+            if c == CHUNKS - 1 and n >= TILES - 2:
+                nc.sync.dma_start(out=out_hbm[:, n, columns(c)], in_=result[:, n % 2, :])
+            elif n % 2 == 1:
+                nc.sync.dma_start(out=out_hbm[:, n - 1 : n + 1, columns(c)], in_=result[:])
+
+        def second(c, n):
+            finish_tile(second_tile(psum_b, c, n), c, n)
+
+        def basis_tiles(first, end):
+            banks = [turn_basis(psum_a, n) for n in range(first, end)]
+            for n in range(first, end):
+                empty_basis(nc.scalar.copy, banks[n - first], n)
+
+        def fused(u, q):
+            empty_quarter(first_quarter(psum_b, u, q), u, q)
+
+        def piece(u, first=0, end=4):
+            for x in range(first, end):
+                first_bank(psum_a, u, x)
+
+        def tiles(c, first, end):
+            for n in range(first, end):
+                second(c, n)
 
         with tc.manual_schedule():
-            nc.vector.tensor_copy(out=mean_f32[:], in_=mean_in[:])
-            nc.vector.tensor_copy(out=rnorm_f32[:], in_=rnorm_in[:])
+            nc.sync.dma_start(out=byte_scale[:], in_=noise_scale.rearrange("(p t) o -> p (t o)", t=PACK))
+            load_noise(0, 1)
+            load_noise(1, 2)
+            load_factor(0, 0)
+            load_factor(0, 1)
+            load_factor(1, 0)
+            load_factor(1, 1)
+            nc.scalar.dma_start(out=mean_cols[:], in_=mean.rearrange("(g p t) -> p g t", g=PASSES, t=PACK))
+            load_noise(2, 3)
+            load_basis(0, 2)
+            load_basis(2, 4)
+            load_noise(3, 5)
+            load_basis(4, 6)
+            load_basis(6, 8)
+            load_amp(0, 2)
+            nc.sync.dma_start(out=rnorm_cols[:], in_=rnorm.rearrange("(p n) -> p n", n=TILES))
+            load_amp(2, 5)
+            make_identity(nc, identity[:])
 
             widen_noise("vector", 0)
-            weave_noise("vector", 0, 0)
-            weave_noise("vector", 0, 1)
+            noise_woven[0] = woven_tile("woven_v", 5)
+            weave_noise("vector", 0, 0, HALF)
+            widen_noise("vector", 1, 0, 2)
+            widen_noise("scalar", 1, 2, 4)
             quantize_noise(0)
+            noise_woven[1] = woven_tile("woven_v", 5)
+            factor_woven[0] = woven_tile("woven_v", 5)
+            factor_woven[1] = woven_tile("ring_a", 1)
             turned = {}
             for g in range(PASSES):
                 for a in range(2):
-                    turned[g, a] = turn_factor(g, a)
-            empty_factor(nc.scalar.copy, turned[0, 0], 0, 0)
-            empty_factor(nc.scalar.copy, turned[0, 1], 0, 1)
+                    turned[g, a] = turn_factor(psum_a, g, a)
+            for g in range(PASSES):
+                for a in range(2):
+                    empty_factor(nc.scalar.copy, turned[g, a], g, a)
+            weave_noise("vector", 1, 0, BANK)
             quantize_factor(0)
-            empty_factor(nc.scalar.copy, turned[1, 0], 1, 0)
-            empty_factor(nc.vector.tensor_copy, turned[1, 1], 1, 1)
-            quantize_factor(1)
-
-            basis_bank = {}
-            for g in range(PASSES):
-                w_tiles(0, g)
-                for quarter in range(4):
-                    empty_woven(first_woven(g, quarter), g, quarter)
-                if g == 0:
-                    for n in range(2):
-                        basis_bank[n] = turn_basis(n)
-            for g in range(PASSES):
-                quantize_w(0, g, whole)
-
-            widen_noise("scalar", 1)
-            weave_noise("gpsimd", 1, 0)
-            weave_noise("gpsimd", 1, 1)
             quantize_noise(1)
+            quantize_factor(1)
+            w_woven[0] = woven_tile("woven_v", 5)
+            w_woven[1] = woven_tile("woven_v", 5)
+            w_woven[2] = woven_tile("ring_c", 1)
             widen_noise("scalar", 2)
-            weave_noise("gpsimd", 2, 0)
-            weave_noise("vector", 2, 1)
-
-            for n in range(TILES):
-                if n >= 2:
-                    basis_bank[n] = turn_basis(n)
-                empty_basis(basis_bank[n], n)
-                if n % 2 == 1:
-                    quantize_basis(n - 1)
+            noise_woven[2] = woven_tile("ring_a", 1)
+            weave_noise("gpsimd", 2, 0, BANK)
+            widen_noise("scalar", 3)
+            widen_noise("scalar", 4)
+            noise_woven[3] = woven_tile("ring_b", 1)
+            weave_noise("gpsimd", 3, 0, BANK)
+            fused(0, 0)
+            fused(0, 1)
+            fused(1, 0)
+            fused(1, 1)
+            fused(0, 2)
+            fused(0, 3)
+            basis_tiles(0, 2)
+            fused(1, 2)
+            fused(1, 3)
+            fused(2, 0)
+            basis_tiles(2, 4)
+            fused(2, 1)
+            fused(2, 2)
+            fused(2, 3)
+            basis_tiles(4, 8)
             quantize_noise(2)
-
-            issued = 0
-            for s in range(CHUNKS * TILES):
-                if s == 5:
-                    widen_noise("scalar", 3)
-                while issued < FIRST_ISSUED[min(s, len(FIRST_ISSUED) - 1)]:
-                    c, bank_of_chunk = divmod(issued, PASSES * PACK)
-                    g, t = divmod(bank_of_chunk, PACK)
-                    first_plane(c + 1, g, t)
-                    issued += 1
-
-                if s == 0:
-                    for half in range(2):
-                        weave_w("vector", 1, 0, half)
-                    for half in range(2):
-                        quantize_w(1, 0, halves[half])
-                if s == 3:
-                    weave_w("gpsimd", 1, 1, 0)
-                    weave_w("vector", 1, 1, 1)
-                    for half in range(2):
-                        quantize_w(1, 1, halves[half])
-                if s == 11:
-                    for half in range(2):
-                        weave_noise("gpsimd", 3, half)
-                    quantize_noise(3)
-                if s == 14:
-                    for engine, g in (("scalar", 1), ("gpsimd", 0)):
-                        weave_w(engine, 2, g, 1)
-                        weave_w(engine, 2, g, 0)
-                        quantize_w(2, g, whole)
-                if s == 22:
-                    for g, engines in enumerate((("gpsimd", "scalar"), ("scalar", "gpsimd"))):
-                        for half in range(2):
-                            weave_w(engines[half], 3, g, half)
-                        quantize_w(3, g, whole)
-
-                finish_tile(s, second_tile(s))
+            quantize_w(0)
+            quantize_basis(0, 4)
+            piece(3)
+            quantize_noise(3)
+            quantize_w(1)
+            tiles(0, 0, 2)
+            piece(4, 0, 2)
+            tiles(0, 2, 4)
+            piece(4, 2, 4)
+            piece(5)
+            quantize_basis(4, 8)
+            quantize_w(2)
+            w_woven[3] = woven_tile("ring_c", 1)
+            weave_w("gpsimd", 3, 0, BANK)
+            noise_woven[4] = woven_tile("ring_a", 1)
+            weave_noise("gpsimd", 4, 0, HALF)
+            tiles(0, 4, 8)
+            w_woven[4] = woven_tile("woven_v", 5)
+            weave_w("scalar", 4, 0, BANK)
+            tiles(1, 0, 6)
+            piece(6)
+            quantize_noise(4)
+            quantize_w(4)
+            quantize_w(3)
+            w_woven[5] = woven_tile("ring_c", 1)
+            weave_w("gpsimd", 5, 0, BANK)
+            w_woven[6] = woven_tile("woven_v", 5)
+            weave_w("gpsimd", 6, 0, P)
+            weave_w("scalar", 6, P, BANK)
+            tiles(1, 6, 8)
+            tiles(2, 0, 6)
+            piece(7)
+            quantize_w(6)
+            quantize_w(5)
+            w_woven[7] = woven_tile("ring_c", 1)
+            weave_w("gpsimd", 7, 0, HALF)
+            weave_w("scalar", 7, HALF, BANK)
+            tiles(2, 6, 8)
+            tiles(3, 0, 6)
+            quantize_w(7)
+            tiles(3, 6, 8)
+            tiles(4, 0, 8)

@@ -258,25 +258,28 @@ def tile_promp_trajectory_sampling_s7_kernel(
 
         results = {}
 
+        def second_pass(bank, c, n, g):
+            u, at = piece_of(c, g)
+            phases = slice(P * g, P * (g + 1))
+            nc.tensor.matmul_mx(
+                out=bank[:],
+                lhsT=basis_codes[:, n, phases].bitcast(FP8X4),
+                lhsT_scale=basis_scales[:, n, phases],
+                rhs=w_codes[u][:, at : at + WIDTHS[c]].bitcast(FP8X4),
+                rhs_scale=w_scales[u][:, at : at + WIDTHS[c]],
+                start=(g == 0),
+                stop=(g == PASSES - 1),
+            )
+
         def second_tile(pool, c, n):
             bank = pool.tile([P, WIDTHS[c]], F32, name="bank")
             for g in range(PASSES):
-                u, at = piece_of(c, g)
-                phases = slice(P * g, P * (g + 1))
-                nc.tensor.matmul_mx(
-                    out=bank[:],
-                    lhsT=basis_codes[:, n, phases].bitcast(FP8X4),
-                    lhsT_scale=basis_scales[:, n, phases],
-                    rhs=w_codes[u][:, at : at + WIDTHS[c]].bitcast(FP8X4),
-                    rhs_scale=w_scales[u][:, at : at + WIDTHS[c]],
-                    start=(g == 0),
-                    stop=(g == PASSES - 1),
-                )
+                second_pass(bank, c, n, g)
             return bank
 
         def finish_tile(bank, c, n):
             if n % 2 == 0:
-                results[c, n // 2] = stage.tile([P, 2, WIDTHS[c]], F32, name="result", bufs=6)
+                results[c, n // 2] = stage.tile([P, 2, WIDTHS[c]], F32, name="result", bufs=8)
             result = results[c, n // 2]
             nc.vector.scalar_tensor_tensor(
                 out=result[:, n % 2, :],
@@ -310,6 +313,23 @@ def tile_promp_trajectory_sampling_s7_kernel(
             for n in range(first, end):
                 second(c, n)
 
+        ahead = {}
+
+        def multiply(c, first, end):
+            for n in range(first, end):
+                ahead[c, n] = second_tile(psum_b, c, n)
+
+        def multiply_by_pass(c, first, end):
+            for n in range(first, end):
+                ahead[c, n] = psum_b.tile([P, WIDTHS[c]], F32, name="bank")
+                second_pass(ahead[c, n], c, n, 0)
+            for n in range(first, end):
+                second_pass(ahead[c, n], c, n, 1)
+
+        def finish(c, first, end):
+            for n in range(first, end):
+                finish_tile(ahead[c, n], c, n)
+
         with tc.manual_schedule():
             nc.sync.dma_start(out=byte_scale[:], in_=noise_scale.rearrange("(p t) o -> p (t o)", t=PACK))
             load_noise(0, 1)
@@ -329,6 +349,15 @@ def tile_promp_trajectory_sampling_s7_kernel(
             nc.sync.dma_start(out=rnorm_cols[:], in_=rnorm.rearrange("(p n) -> p n", n=TILES))
             load_amp(2, 5)
             make_identity(nc, identity[:])
+            idle_in = keep.tile([P, BANK], BF16, name="idle_in")
+            nc.gpsimd.memset(idle_in[:], 0.0)
+            idle_out = psum_a.tile([P, BANK], F32, name="bank")
+
+            def warm_up(count):
+                for repeat in range(count):
+                    nc.tensor.matmul(idle_out[:], lhsT=idle_in[:, :P], rhs=idle_in[:], start=True, stop=True)
+
+            warm_up(4)
 
             widen_noise("vector", 0)
             noise_woven[0] = woven_tile("woven_v", 5)
@@ -343,6 +372,8 @@ def tile_promp_trajectory_sampling_s7_kernel(
             for g in range(PASSES):
                 for a in range(2):
                     turned[g, a] = turn_factor(psum_a, g, a)
+                    warm_up(1)
+            warm_up(1)
             for g in range(PASSES):
                 for a in range(2):
                     empty_factor(nc.scalar.copy, turned[g, a], g, a)
@@ -392,29 +423,36 @@ def tile_promp_trajectory_sampling_s7_kernel(
             weave_w("gpsimd", 3, 0, BANK)
             noise_woven[4] = woven_tile("ring_a", 1)
             weave_noise("gpsimd", 4, 0, HALF)
-            tiles(0, 4, 8)
-            w_woven[4] = woven_tile("woven_v", 5)
+            w_woven[4] = woven_tile("ring_b", 1)
             weave_w("scalar", 4, 0, BANK)
+            tiles(0, 4, 8)
             tiles(1, 0, 6)
+            multiply(1, 6, 8)
             piece(6)
             quantize_noise(4)
-            quantize_w(4)
             quantize_w(3)
-            w_woven[5] = woven_tile("ring_c", 1)
+            quantize_w(4)
+            w_woven[5] = woven_tile("ring_b", 1)
             weave_w("gpsimd", 5, 0, BANK)
-            w_woven[6] = woven_tile("woven_v", 5)
+            w_woven[6] = woven_tile("ring_a", 1)
             weave_w("gpsimd", 6, 0, P)
             weave_w("scalar", 6, P, BANK)
-            tiles(1, 6, 8)
-            tiles(2, 0, 6)
+            multiply_by_pass(2, 0, 2)
+            finish(1, 6, 8)
+            finish(2, 0, 2)
+            tiles(2, 2, 6)
+            multiply(2, 6, 8)
             piece(7)
-            quantize_w(6)
             quantize_w(5)
-            w_woven[7] = woven_tile("ring_c", 1)
+            quantize_w(6)
+            w_woven[7] = woven_tile("ring_a", 1)
             weave_w("gpsimd", 7, 0, HALF)
             weave_w("scalar", 7, HALF, BANK)
-            tiles(2, 6, 8)
-            tiles(3, 0, 6)
+            multiply_by_pass(3, 0, 2)
+            finish(2, 6, 8)
+            finish(3, 0, 2)
+            tiles(3, 2, 4)
+            multiply(3, 4, 8)
             quantize_w(7)
-            tiles(3, 6, 8)
+            finish(3, 4, 8)
             tiles(4, 0, 8)

@@ -262,7 +262,7 @@ def tile_promp_trajectory_sampling_s7_kernel(
             u, at = piece_of(c, g)
             phases = slice(P * g, P * (g + 1))
             nc.tensor.matmul_mx(
-                out=bank[:],
+                out=bank,
                 lhsT=basis_codes[:, n, phases].bitcast(FP8X4),
                 lhsT_scale=basis_scales[:, n, phases],
                 rhs=w_codes[u][:, at : at + WIDTHS[c]].bitcast(FP8X4),
@@ -271,31 +271,22 @@ def tile_promp_trajectory_sampling_s7_kernel(
                 stop=(g == PASSES - 1),
             )
 
-        def second_tile(pool, c, n):
-            bank = pool.tile([P, WIDTHS[c]], F32, name="bank")
-            for g in range(PASSES):
-                second_pass(bank, c, n, g)
-            return bank
-
         def finish_tile(bank, c, n):
             if n % 2 == 0:
                 results[c, n // 2] = stage.tile([P, 2, WIDTHS[c]], F32, name="result", bufs=8)
             result = results[c, n // 2]
             nc.vector.scalar_tensor_tensor(
                 out=result[:, n % 2, :],
-                in0=bank[:],
+                in0=bank,
                 scalar=rnorm_cols[:, n : n + 1],
                 in1=amp_rows[c],
                 op0=MULT,
                 op1=MULT,
             )
-            if c == CHUNKS - 1 and n >= TILES - 2:
+            if (c == 3 and n >= 4) or (c == 4 and n >= 6):
                 nc.sync.dma_start(out=out_hbm[:, n, columns(c)], in_=result[:, n % 2, :])
             elif n % 2 == 1:
                 nc.sync.dma_start(out=out_hbm[:, n - 1 : n + 1, columns(c)], in_=result[:])
-
-        def second(c, n):
-            finish_tile(second_tile(psum_b, c, n), c, n)
 
         def basis_tiles(first, end):
             banks = [turn_basis(psum_a, n) for n in range(first, end)]
@@ -310,18 +301,26 @@ def tile_promp_trajectory_sampling_s7_kernel(
                 first_bank(psum_a, u, x)
 
         def tiles(c, first, end):
-            for n in range(first, end):
-                second(c, n)
+            step = BANK // WIDTHS[c]
+            for n in range(first, end, step):
+                multiply(c, n, n + step)
+                finish(c, n, n + step)
 
         ahead = {}
 
         def multiply(c, first, end):
             for n in range(first, end):
-                ahead[c, n] = second_tile(psum_b, c, n)
+                if WIDTHS[c] == BANK:
+                    ahead[c, n] = psum_b.tile([P, BANK], F32, name="bank")[:]
+                elif n % 2 == 0:
+                    both = psum_b.tile([P, 2, HALF], F32, name="bank")
+                    ahead[c, n], ahead[c, n + 1] = both[:, 0, :], both[:, 1, :]
+                for g in range(PASSES):
+                    second_pass(ahead[c, n], c, n, g)
 
         def multiply_by_pass(c, first, end):
             for n in range(first, end):
-                ahead[c, n] = psum_b.tile([P, WIDTHS[c]], F32, name="bank")
+                ahead[c, n] = psum_b.tile([P, BANK], F32, name="bank")[:]
                 second_pass(ahead[c, n], c, n, 0)
             for n in range(first, end):
                 second_pass(ahead[c, n], c, n, 1)
@@ -331,8 +330,8 @@ def tile_promp_trajectory_sampling_s7_kernel(
                 finish_tile(ahead[c, n], c, n)
 
         with tc.manual_schedule():
-            nc.sync.dma_start(out=byte_scale[:], in_=noise_scale.rearrange("(p t) o -> p (t o)", t=PACK))
             load_noise(0, 1)
+            nc.scalar.dma_start(out=byte_scale[:], in_=noise_scale.rearrange("(p t) o -> p (t o)", t=PACK))
             load_noise(1, 2)
             load_factor(0, 0)
             load_factor(0, 1)
@@ -349,15 +348,6 @@ def tile_promp_trajectory_sampling_s7_kernel(
             nc.sync.dma_start(out=rnorm_cols[:], in_=rnorm.rearrange("(p n) -> p n", n=TILES))
             load_amp(2, 5)
             make_identity(nc, identity[:])
-            idle_in = keep.tile([P, BANK], BF16, name="idle_in")
-            nc.gpsimd.memset(idle_in[:], 0.0)
-            idle_out = psum_a.tile([P, BANK], F32, name="bank")
-
-            def warm_up(count):
-                for repeat in range(count):
-                    nc.tensor.matmul(idle_out[:], lhsT=idle_in[:, :P], rhs=idle_in[:], start=True, stop=True)
-
-            warm_up(4)
 
             widen_noise("vector", 0)
             noise_woven[0] = woven_tile("woven_v", 5)
@@ -372,8 +362,6 @@ def tile_promp_trajectory_sampling_s7_kernel(
             for g in range(PASSES):
                 for a in range(2):
                     turned[g, a] = turn_factor(psum_a, g, a)
-                    warm_up(1)
-            warm_up(1)
             for g in range(PASSES):
                 for a in range(2):
                     empty_factor(nc.scalar.copy, turned[g, a], g, a)
@@ -397,12 +385,12 @@ def tile_promp_trajectory_sampling_s7_kernel(
             fused(1, 1)
             fused(0, 2)
             fused(0, 3)
-            basis_tiles(0, 2)
             fused(1, 2)
             fused(1, 3)
+            basis_tiles(0, 2)
             fused(2, 0)
-            basis_tiles(2, 4)
             fused(2, 1)
+            basis_tiles(2, 4)
             fused(2, 2)
             fused(2, 3)
             basis_tiles(4, 8)
@@ -410,29 +398,36 @@ def tile_promp_trajectory_sampling_s7_kernel(
             quantize_w(0)
             quantize_basis(0, 4)
             piece(3)
-            quantize_noise(3)
+            multiply(0, 0, 4)
             quantize_w(1)
-            tiles(0, 0, 2)
-            piece(4, 0, 2)
-            tiles(0, 2, 4)
-            piece(4, 2, 4)
-            piece(5)
-            quantize_basis(4, 8)
             quantize_w(2)
-            w_woven[3] = woven_tile("ring_c", 1)
+            finish(0, 0, 4)
+            piece(4, 0, 2)
+            multiply(1, 0, 2)
+            piece(4, 2, 4)
+            multiply(1, 2, 4)
+            quantize_basis(4, 8)
+            quantize_noise(3)
+            w_woven[3] = woven_tile("ring_b", 1)
             weave_w("gpsimd", 3, 0, BANK)
             noise_woven[4] = woven_tile("ring_a", 1)
             weave_noise("gpsimd", 4, 0, HALF)
-            w_woven[4] = woven_tile("ring_b", 1)
+            w_woven[4] = woven_tile("ring_c", 1)
             weave_w("scalar", 4, 0, BANK)
-            tiles(0, 4, 8)
-            tiles(1, 0, 6)
-            multiply(1, 6, 8)
+            finish(1, 0, 2)
+            multiply(0, 4, 8)
+            finish(1, 2, 4)
+            piece(5, 0, 2)
+            multiply(1, 4, 5)
+            piece(5, 2, 4)
+            finish(0, 4, 8)
+            multiply(1, 5, 8)
+            finish(1, 4, 6)
             piece(6)
             quantize_noise(4)
             quantize_w(3)
             quantize_w(4)
-            w_woven[5] = woven_tile("ring_b", 1)
+            w_woven[5] = woven_tile("ring_c", 1)
             weave_w("gpsimd", 5, 0, BANK)
             w_woven[6] = woven_tile("ring_a", 1)
             weave_w("gpsimd", 6, 0, P)
@@ -451,8 +446,8 @@ def tile_promp_trajectory_sampling_s7_kernel(
             multiply_by_pass(3, 0, 2)
             finish(2, 6, 8)
             finish(3, 0, 2)
-            tiles(3, 2, 4)
-            multiply(3, 4, 8)
+            tiles(3, 2, 5)
+            multiply(3, 5, 8)
             quantize_w(7)
-            finish(3, 4, 8)
+            finish(3, 5, 8)
             tiles(4, 0, 8)

@@ -83,12 +83,11 @@ def tile_promp_trajectory_sampling_s7_kernel(
             factor_rows[g, a] = keep.tile([P, 2, R], BF16, name=f"factor_rows_{g}_{a}")
             nc.sync.dma_start(out=factor_rows[g, a][:], in_=factor_hbm[g][:, 2 * a : 2 * a + 2, :])
 
-        def load_noise(first, end):
-            lo, hi = STARTS[first], STARTS[end - 1] + WIDTHS[end - 1]
-            bytes_in = keep.tile([P, PACK, hi - lo], U8, name=f"noise_in_{first}")
+        def load_noise(lo, hi):
+            bytes_in = keep.tile([P, PACK, hi - lo], U8, name=f"noise_in_{lo}")
             nc.sync.dma_start(out=bytes_in[:], in_=noise_hbm[:, :, lo:hi])
-            for c in range(first, end):
-                noise_in[c] = bytes_in[:, :, STARTS[c] - lo : STARTS[c] - lo + WIDTHS[c]]
+            for j in range(lo, hi, HALF):
+                noise_in[j] = (bytes_in, lo)
 
         def load_basis(first, end):
             rows = keep.tile([P, end - first, B], BF16, name=f"basis_rows_{first}")
@@ -166,12 +165,14 @@ def tile_promp_trajectory_sampling_s7_kernel(
         noise_planes = {}
         noise_woven = {}
 
-        def widen_noise(engine, c, first=0, end=PACK):
+        def widen_noise(engine, c, first=0, end=PACK, lo=0, hi=None):
             if c not in noise_planes:
                 noise_planes[c] = stage.tile([P, PACK, WIDTHS[c]], BF16, name="noise_planes", bufs=4)
+            hi = hi or WIDTHS[c]
+            bytes_in, base = noise_in[STARTS[c] + lo]
             for t in range(first, end):
-                src = noise_in[c][:, t, :].bitcast(FP8)
-                dst = noise_planes[c][:, t, :]
+                src = bytes_in[:, t, STARTS[c] + lo - base : STARTS[c] + hi - base].bitcast(FP8)
+                dst = noise_planes[c][:, t, lo:hi]
                 scale = byte_scale[:, t : t + 1]
                 if engine == "scalar":
                     nc.scalar.activation(out=dst, in_=src, func=COPY, scale=scale)
@@ -283,7 +284,7 @@ def tile_promp_trajectory_sampling_s7_kernel(
                 op0=MULT,
                 op1=MULT,
             )
-            if (c == 3 and n >= 4) or (c == 4 and n >= 6):
+            if c in (1, 2, 3) or (c == 4 and n >= 6):
                 nc.sync.dma_start(out=out_hbm[:, n, columns(c)], in_=result[:, n % 2, :])
             elif n % 2 == 1:
                 nc.sync.dma_start(out=out_hbm[:, n - 1 : n + 1, columns(c)], in_=result[:])
@@ -330,18 +331,16 @@ def tile_promp_trajectory_sampling_s7_kernel(
                 finish_tile(ahead[c, n], c, n)
 
         with tc.manual_schedule():
-            load_noise(0, 1)
+            load_noise(0, 768)
             nc.scalar.dma_start(out=byte_scale[:], in_=noise_scale.rearrange("(p t) o -> p (t o)", t=PACK))
-            load_noise(1, 2)
             load_factor(0, 0)
             load_factor(0, 1)
             load_factor(1, 0)
             load_factor(1, 1)
             nc.scalar.dma_start(out=mean_cols[:], in_=mean.rearrange("(g p t) -> p g t", g=PASSES, t=PACK))
-            load_noise(2, 3)
+            load_noise(768, 2048)
             load_basis(0, 2)
             load_basis(2, 4)
-            load_noise(3, 5)
             load_basis(4, 6)
             load_basis(6, 8)
             load_amp(0, 2)

@@ -273,21 +273,21 @@ def tile_promp_trajectory_sampling_s7_kernel(
             )
 
         def finish_tile(bank, c, n):
-            if n % 2 == 0:
-                results[c, n // 2] = stage.tile([P, 2, WIDTHS[c]], F32, name="result", bufs=8)
-            result = results[c, n // 2]
+            group = 2 * BANK // WIDTHS[c]
+            first = n - n % group
+            if n == first:
+                results[c, first] = stage.tile([P, group, WIDTHS[c]], F32, name=f"result_{group * WIDTHS[c]}", bufs=8)
+            result = results[c, first]
             nc.vector.scalar_tensor_tensor(
-                out=result[:, n % 2, :],
+                out=result[:, n - first, :],
                 in0=bank,
                 scalar=rnorm_cols[:, n : n + 1],
                 in1=amp_rows[c],
                 op0=MULT,
                 op1=MULT,
             )
-            if c in (1, 2, 3) or (c == 4 and n >= 6):
-                nc.sync.dma_start(out=out_hbm[:, n, columns(c)], in_=result[:, n % 2, :])
-            elif n % 2 == 1:
-                nc.sync.dma_start(out=out_hbm[:, n - 1 : n + 1, columns(c)], in_=result[:])
+            if n == first + group - 1:
+                nc.sync.dma_start(out=out_hbm[:, first : first + group, columns(c)], in_=result[:])
 
         def basis_tiles(first, end):
             banks = [turn_basis(psum_a, n) for n in range(first, end)]
@@ -382,10 +382,10 @@ def tile_promp_trajectory_sampling_s7_kernel(
             fused(0, 1)
             fused(1, 0)
             fused(1, 1)
-            fused(0, 2)
-            fused(0, 3)
             fused(1, 2)
             fused(1, 3)
+            fused(0, 2)
+            fused(0, 3)
             basis_tiles(0, 2)
             fused(2, 0)
             fused(2, 1)

@@ -350,9 +350,9 @@ def tile_promp_trajectory_sampling_s7_kernel(
 
             widen_noise("vector", 0)
             noise_woven[0] = woven_tile("woven_v", 5)
+            widen_noise("vector", 1, 0, 1)
             weave_noise("vector", 0, 0, HALF)
-            widen_noise("vector", 1, 0, 2)
-            widen_noise("scalar", 1, 2, 4)
+            widen_noise("scalar", 1, 1, 4)
             quantize_noise(0)
             noise_woven[1] = woven_tile("woven_v", 5)
             factor_woven[0] = woven_tile("woven_v", 5)
@@ -371,19 +371,20 @@ def tile_promp_trajectory_sampling_s7_kernel(
             w_woven[0] = woven_tile("woven_v", 5)
             w_woven[1] = woven_tile("woven_v", 5)
             w_woven[2] = woven_tile("ring_c", 1)
-            widen_noise("scalar", 2)
             noise_woven[2] = woven_tile("ring_a", 1)
-            weave_noise("gpsimd", 2, 0, BANK)
+            for lo in (0, HALF):
+                widen_noise("scalar", 2, 0, 4, lo, lo + HALF)
+                weave_noise("gpsimd", 2, lo, lo + HALF)
             widen_noise("scalar", 3)
-            widen_noise("scalar", 4)
-            noise_woven[3] = woven_tile("ring_b", 1)
-            weave_noise("gpsimd", 3, 0, BANK)
             fused(0, 0)
             fused(0, 1)
             fused(1, 0)
             fused(1, 1)
             fused(1, 2)
             fused(1, 3)
+            quantize_noise(2)
+            noise_woven[3] = woven_tile("ring_a", 1)
+            weave_noise("gpsimd", 3, 0, BANK)
             fused(0, 2)
             fused(0, 3)
             basis_tiles(0, 2)
@@ -392,12 +393,14 @@ def tile_promp_trajectory_sampling_s7_kernel(
             basis_tiles(2, 4)
             fused(2, 2)
             fused(2, 3)
-            basis_tiles(4, 8)
-            quantize_noise(2)
+            piece(3, 0, 2)
+            basis_tiles(4, 6)
+            piece(3, 2, 4)
+            basis_tiles(6, 8)
             quantize_w(0)
             quantize_basis(0, 4)
-            piece(3)
             multiply(0, 0, 4)
+            widen_noise("scalar", 4)
             quantize_w(1)
             quantize_w(2)
             finish(0, 0, 4)
@@ -407,9 +410,9 @@ def tile_promp_trajectory_sampling_s7_kernel(
             multiply(1, 2, 4)
             quantize_basis(4, 8)
             quantize_noise(3)
-            w_woven[3] = woven_tile("ring_b", 1)
+            w_woven[3] = woven_tile("ring_a", 1)
             weave_w("gpsimd", 3, 0, BANK)
-            noise_woven[4] = woven_tile("ring_a", 1)
+            noise_woven[4] = woven_tile("ring_b", 1)
             weave_noise("gpsimd", 4, 0, HALF)
             w_woven[4] = woven_tile("ring_c", 1)
             weave_w("scalar", 4, 0, BANK)
@@ -428,7 +431,7 @@ def tile_promp_trajectory_sampling_s7_kernel(
             quantize_w(4)
             w_woven[5] = woven_tile("ring_c", 1)
             weave_w("gpsimd", 5, 0, BANK)
-            w_woven[6] = woven_tile("ring_a", 1)
+            w_woven[6] = woven_tile("ring_b", 1)
             weave_w("gpsimd", 6, 0, P)
             weave_w("scalar", 6, P, BANK)
             multiply_by_pass(2, 0, 2)
@@ -439,7 +442,7 @@ def tile_promp_trajectory_sampling_s7_kernel(
             piece(7)
             quantize_w(5)
             quantize_w(6)
-            w_woven[7] = woven_tile("ring_a", 1)
+            w_woven[7] = woven_tile("ring_b", 1)
             weave_w("gpsimd", 7, 0, HALF)
             weave_w("scalar", 7, HALF, BANK)
             multiply_by_pass(3, 0, 2)

@@ -347,6 +347,9 @@ def tile_promp_trajectory_sampling_s7_kernel(
             nc.sync.dma_start(out=rnorm_cols[:], in_=rnorm.rearrange("(p n) -> p n", n=TILES))
             load_amp(2, 5)
             make_identity(nc, identity[:])
+            table_in = keep.tile([P, 1], F32, name="table_in")
+            nc.vector.memset(table_in[:], 0.0)
+            nc.scalar.activation(out=table_in[:], in_=table_in[:], func=IDENTITY)
 
             widen_noise("vector", 0)
             noise_woven[0] = woven_tile("woven_v", 5)

@@ -56,7 +56,7 @@ def tile_promp_trajectory_sampling_s7_kernel(
         factor_woven = {}
         factor_codes = keep.tile([P, PASSES, PACK * P], U32, name="factor_codes", align_bytes=64)
         factor_scales = keep.tile([P, PASSES, PACK * P], U8, name="factor_scales", align_bytes=64)
-        basis_woven = keep.tile([P, TILES, PASSES, P, PACK], BF16, name="basis_woven", align_bytes=64)
+        basis_woven = {}
         basis_codes = keep.tile([P, TILES, PASSES * P], U32, name="basis_codes", align_bytes=64)
         basis_scales = keep.tile([P, TILES, PASSES * P], U8, name="basis_scales", align_bytes=64)
         noise_codes = keep.tile([P, N], U32, name="noise_codes", align_bytes=64)
@@ -134,7 +134,11 @@ def tile_promp_trajectory_sampling_s7_kernel(
             return bank
 
         def empty_basis(copy, bank, n):
-            woven = basis_woven[:, n].rearrange("p g m t -> p (g m t)").bitcast(F32)
+            if n % 4 == 0:
+                basis_woven[n // 4] = stage.tile(
+                    [P, 4, PASSES, P, PACK], BF16, name=f"basis_woven_{n // 4}", align_bytes=64, bufs=1
+                )
+            woven = basis_woven[n // 4][:, n % 4].rearrange("p g m t -> p (g m t)").bitcast(F32)
             copy(
                 out=woven.rearrange("p (g m u) -> p g m u", g=PASSES, u=2),
                 in_=bank[:].rearrange("p g u m -> p g m u"),
@@ -145,7 +149,7 @@ def tile_promp_trajectory_sampling_s7_kernel(
             nc.vector.quantize_mx(
                 out=basis_codes[:, some].rearrange("p n k -> p (n k)").bitcast(FP8X4),
                 scales=basis_scales[:, some].rearrange("p n k -> p (n k)"),
-                in_=basis_woven[:, some].rearrange("p n g m t -> p (n g m t)"),
+                in_=basis_woven[first // 4][:].rearrange("p n g m t -> p (n g m t)"),
             )
 
         def weave(engine, woven, planes, first, end):
@@ -287,7 +291,8 @@ def tile_promp_trajectory_sampling_s7_kernel(
                 op1=MULT,
             )
             if n == first + group - 1:
-                nc.sync.dma_start(out=out_hbm[:, first : first + group, columns(c)], in_=result[:])
+                queue = nc.scalar if (c, first) in ((3, 2), (3, 6), (4, 4)) else nc.sync
+                queue.dma_start(out=out_hbm[:, first : first + group, columns(c)], in_=result[:])
 
         def basis_tiles(first, end):
             banks = [turn_basis(psum_a, n) for n in range(first, end)]
@@ -385,14 +390,15 @@ def tile_promp_trajectory_sampling_s7_kernel(
             fused(1, 1)
             fused(1, 2)
             fused(1, 3)
+            fused(0, 2)
             quantize_noise(2)
             noise_woven[3] = woven_tile("ring_a", 1)
-            weave_noise("gpsimd", 3, 0, BANK)
-            fused(0, 2)
+            weave_noise("gpsimd", 3, 0, 3 * P)
             fused(0, 3)
             basis_tiles(0, 2)
             fused(2, 0)
             fused(2, 1)
+            weave_noise("scalar", 3, 3 * P, BANK)
             basis_tiles(2, 4)
             fused(2, 2)
             fused(2, 3)
@@ -406,14 +412,14 @@ def tile_promp_trajectory_sampling_s7_kernel(
             widen_noise("scalar", 4)
             quantize_w(1)
             quantize_w(2)
+            quantize_noise(3)
             finish(0, 0, 4)
             piece(4, 0, 2)
             multiply(1, 0, 2)
             piece(4, 2, 4)
             multiply(1, 2, 4)
             quantize_basis(4, 8)
-            quantize_noise(3)
-            w_woven[3] = woven_tile("ring_a", 1)
+            w_woven[3] = woven_tile("basis_woven_1", 1)
             weave_w("gpsimd", 3, 0, BANK)
             noise_woven[4] = woven_tile("ring_b", 1)
             weave_noise("gpsimd", 4, 0, HALF)
@@ -423,21 +429,22 @@ def tile_promp_trajectory_sampling_s7_kernel(
             multiply(0, 4, 8)
             finish(1, 2, 4)
             piece(5, 0, 2)
-            multiply(1, 4, 5)
-            piece(5, 2, 4)
+            multiply(1, 4, 6)
             finish(0, 4, 8)
-            multiply(1, 5, 8)
+            piece(5, 2, 4)
+            multiply(1, 6, 8)
             finish(1, 4, 6)
-            piece(6)
+            piece(6, 0, 2)
             quantize_noise(4)
             quantize_w(3)
             quantize_w(4)
             w_woven[5] = woven_tile("ring_c", 1)
             weave_w("gpsimd", 5, 0, BANK)
+            multiply_by_pass(2, 0, 2)
+            piece(6, 2, 4)
             w_woven[6] = woven_tile("ring_b", 1)
             weave_w("gpsimd", 6, 0, P)
             weave_w("scalar", 6, P, BANK)
-            multiply_by_pass(2, 0, 2)
             finish(1, 6, 8)
             finish(2, 0, 2)
             tiles(2, 2, 6)

@@ -280,7 +280,7 @@ def tile_promp_trajectory_sampling_s7_kernel(
             group = 2 * BANK // WIDTHS[c]
             first = n - n % group
             if n == first:
-                results[c, first] = stage.tile([P, group, WIDTHS[c]], F32, name=f"result_{group * WIDTHS[c]}", bufs=8)
+                results[c, first] = stage.tile([P, group, WIDTHS[c]], F32, name="result", bufs=16)
             result = results[c, first]
             nc.vector.scalar_tensor_tensor(
                 out=result[:, n - first, :],

@@ -157,7 +157,12 @@ def tile_promp_trajectory_sampling_s7_kernel(
             src = planes[:, :, first:end]
             if engine == "gpsimd":
                 nc.gpsimd.tensor_scalar(
-                    out=dst, in0=src.rearrange("p t j -> p j t"), scalar1=1.0, scalar2=0.0, op0=MULT, op1=ADD
+                    out=dst.rearrange("p (j i) t -> p j t i", i=4),
+                    in0=src.rearrange("p t (j i) -> p j t i", i=4),
+                    scalar1=1.0,
+                    scalar2=0.0,
+                    op0=MULT,
+                    op1=ADD,
                 )
                 return
             copy = nc.scalar.copy if engine == "scalar" else nc.vector.tensor_copy

@@ -54,13 +54,13 @@ def tile_promp_trajectory_sampling_s7_kernel(
         psum_b = psum_a
 
         factor_woven = {}
-        factor_codes = keep.tile([P, PASSES, PACK * P], U32, name="factor_codes", align_bytes=64)
-        factor_scales = keep.tile([P, PASSES, PACK * P], U8, name="factor_scales", align_bytes=64)
+        factor_codes = keep.tile([P, PASSES, PACK * P], U32, name="factor_codes", align_bytes=256)
+        factor_scales = keep.tile([P, PASSES, PACK * P], U8, name="factor_scales", align_bytes=256)
         basis_woven = {}
-        basis_codes = keep.tile([P, TILES, PASSES * P], U32, name="basis_codes", align_bytes=64)
-        basis_scales = keep.tile([P, TILES, PASSES * P], U8, name="basis_scales", align_bytes=64)
-        noise_codes = keep.tile([P, N], U32, name="noise_codes", align_bytes=64)
-        noise_scales = keep.tile([P, N], U8, name="noise_scales", align_bytes=64)
+        basis_codes = keep.tile([P, TILES, PASSES * P], U32, name="basis_codes", align_bytes=256)
+        basis_scales = keep.tile([P, TILES, PASSES * P], U8, name="basis_scales", align_bytes=256)
+        noise_codes = keep.tile([P, N], U32, name="noise_codes", align_bytes=256)
+        noise_scales = keep.tile([P, N], U8, name="noise_scales", align_bytes=256)
         byte_scale = keep.tile([P, PACK], F32, name="byte_scale")
         mean_cols = keep.tile([P, PASSES, PACK], BF16, name="mean_cols")
         rnorm_cols = keep.tile([P, TILES], BF16, name="rnorm_cols")
@@ -80,24 +80,24 @@ def tile_promp_trajectory_sampling_s7_kernel(
             return slice(STARTS[c], STARTS[c] + WIDTHS[c])
 
         def load_factor(g, a):
-            factor_rows[g, a] = keep.tile([P, 2, R], BF16, name=f"factor_rows_{g}_{a}")
+            factor_rows[g, a] = keep.tile([P, 2, R], BF16, name=f"factor_rows_{g}_{a}", align_bytes=256)
             nc.sync.dma_start(out=factor_rows[g, a][:], in_=factor_hbm[g][:, 2 * a : 2 * a + 2, :])
 
         def load_noise(lo, hi):
-            bytes_in = keep.tile([P, PACK, hi - lo], U8, name=f"noise_in_{lo}")
+            bytes_in = keep.tile([P, PACK, hi - lo], U8, name=f"noise_in_{lo}", align_bytes=256)
             nc.sync.dma_start(out=bytes_in[:], in_=noise_hbm[:, :, lo:hi])
             for j in range(lo, hi, HALF):
                 noise_in[j] = (bytes_in, lo)
 
         def load_basis(first, end):
-            rows = keep.tile([P, end - first, B], BF16, name=f"basis_rows_{first}")
+            rows = keep.tile([P, end - first, B], BF16, name=f"basis_rows_{first}", align_bytes=256)
             nc.sync.dma_start(out=rows[:], in_=basis_hbm[:, first:end, :])
             for n in range(first, end):
                 basis_rows[n] = rows[:, n - first, :]
 
         def load_amp(first, end):
             lo, hi = STARTS[first], STARTS[end - 1] + WIDTHS[end - 1]
-            rows = keep.tile([P, hi - lo], BF16, name=f"amp_rows_{first}")
+            rows = keep.tile([P, hi - lo], BF16, name=f"amp_rows_{first}", align_bytes=256)
             nc.sync.dma_start(out=rows[:], in_=amp[lo:hi].partition_broadcast(P))
             for c in range(first, end):
                 amp_rows[c] = rows[:, STARTS[c] - lo : STARTS[c] - lo + WIDTHS[c]]
@@ -136,7 +136,7 @@ def tile_promp_trajectory_sampling_s7_kernel(
         def empty_basis(copy, bank, n):
             if n % 4 == 0:
                 basis_woven[n // 4] = stage.tile(
-                    [P, 4, PASSES, P, PACK], BF16, name=f"basis_woven_{n // 4}", align_bytes=64, bufs=1
+                    [P, 4, PASSES, P, PACK], BF16, name=f"basis_woven_{n // 4}", align_bytes=256, bufs=1
                 )
             woven = basis_woven[n // 4][:, n % 4].rearrange("p g m t -> p (g m t)").bitcast(F32)
             copy(
@@ -189,7 +189,7 @@ def tile_promp_trajectory_sampling_s7_kernel(
                     nc.vector.tensor_scalar(out=dst, in0=src, scalar1=scale, scalar2=None, op0=MULT)
 
         def woven_tile(tag, bufs):
-            return stage.tile([P, BANK, PACK], BF16, name=tag, align_bytes=64, bufs=bufs)
+            return stage.tile([P, BANK, PACK], BF16, name=tag, align_bytes=256, bufs=bufs)
 
         def weave_noise(engine, c, first, end):
             weave(engine, noise_woven[c], noise_planes[c], first, end)
@@ -258,8 +258,8 @@ def tile_promp_trajectory_sampling_s7_kernel(
             weave(engine, w_woven[u], w_planes[u], first, end)
 
         def quantize_w(u):
-            w_codes[u] = keep.tile([P, BANK], U32, name=f"w_codes_{u}", align_bytes=64)
-            w_scales[u] = keep.tile([P, BANK], U8, name=f"w_scales_{u}", align_bytes=64)
+            w_codes[u] = keep.tile([P, BANK], U32, name=f"w_codes_{u}", align_bytes=256)
+            w_scales[u] = keep.tile([P, BANK], U8, name=f"w_scales_{u}", align_bytes=256)
             nc.vector.quantize_mx(
                 out=w_codes[u][:].bitcast(FP8X4),
                 scales=w_scales[u][:],
@@ -285,7 +285,7 @@ def tile_promp_trajectory_sampling_s7_kernel(
             group = 2 * BANK // WIDTHS[c]
             first = n - n % group
             if n == first:
-                results[c, first] = stage.tile([P, group, WIDTHS[c]], F32, name="result", bufs=16)
+                results[c, first] = stage.tile([P, group, WIDTHS[c]], F32, name="result", bufs=16, align_bytes=256)
             result = results[c, first]
             nc.vector.scalar_tensor_tensor(
                 out=result[:, n - first, :],

@@ -283,6 +283,8 @@ def tile_promp_trajectory_sampling_s7_kernel(
 
         def finish_tile(bank, c, n):
             group = 2 * BANK // WIDTHS[c]
+            if c == CHUNKS - 1 and n >= TILES - group:
+                group = group // 2
             first = n - n % group
             if n == first:
                 results[c, first] = stage.tile([P, group, WIDTHS[c]], F32, name="result", bufs=16, align_bytes=256)

@@ -83,11 +83,12 @@ def tile_promp_trajectory_sampling_s7_kernel(
             factor_rows[g, a] = keep.tile([P, 2, R], BF16, name=f"factor_rows_{g}_{a}", align_bytes=256)
             nc.sync.dma_start(out=factor_rows[g, a][:], in_=factor_hbm[g][:, 2 * a : 2 * a + 2, :])
 
-        def load_noise(lo, hi):
-            bytes_in = keep.tile([P, PACK, hi - lo], U8, name=f"noise_in_{lo}", align_bytes=256)
-            nc.sync.dma_start(out=bytes_in[:], in_=noise_hbm[:, :, lo:hi])
+        def load_noise(lo, hi, first=0, end=PACK):
+            bytes_in = keep.tile([P, end - first, hi - lo], U8, name=f"noise_in_{lo}_{first}", align_bytes=256)
+            nc.sync.dma_start(out=bytes_in[:], in_=noise_hbm[:, first:end, lo:hi])
             for j in range(lo, hi, HALF):
-                noise_in[j] = (bytes_in, lo)
+                for t in range(first, end):
+                    noise_in[j, t] = (bytes_in[:, t - first, :], lo)
 
         def load_basis(first, end):
             rows = keep.tile([P, end - first, B], BF16, name=f"basis_rows_{first}", align_bytes=256)
@@ -95,12 +96,18 @@ def tile_promp_trajectory_sampling_s7_kernel(
             for n in range(first, end):
                 basis_rows[n] = rows[:, n - first, :]
 
-        def load_amp(first, end):
-            lo, hi = STARTS[first], STARTS[end - 1] + WIDTHS[end - 1]
-            rows = keep.tile([P, hi - lo], BF16, name=f"amp_rows_{first}", align_bytes=256)
-            nc.sync.dma_start(out=rows[:], in_=amp[lo:hi].partition_broadcast(P))
-            for c in range(first, end):
-                amp_rows[c] = rows[:, STARTS[c] - lo : STARTS[c] - lo + WIDTHS[c]]
+        amp_in = keep.tile([P, 8], BF16, name="amp_in")
+        amp_all = keep.tile([P, N], BF16, name="amp_all", align_bytes=256)
+        for c in range(CHUNKS):
+            amp_rows[c] = amp_all[:, columns(c)]
+
+        def spread_amp():
+            bank = psum_a.tile([P, 4, P], F32, name="bank")
+            words = amp_in[:].bitcast(F32)
+            for m in range(4):
+                nc.tensor.transpose(bank[:, m, :], words[:, m : m + 1].to_broadcast([P, P]), identity[:])
+            words = amp_all[:, : N // 2].bitcast(F32)
+            nc.scalar.copy(out=words.rearrange("p (q m) -> p q m", m=4), in_=bank[:].rearrange("p m q -> p q m"))
 
         def turn_factor(pool, g, a):
             bank = pool.tile([P, 2, 2, P], F32, name="bank")
@@ -117,11 +124,11 @@ def tile_promp_trajectory_sampling_s7_kernel(
                 in_=bank[:].rearrange("p x u m -> p x m u"),
             )
 
-        def quantize_factor(g):
+        def quantize_factor(g, lo=0, hi=BANK):
             nc.vector.quantize_mx(
-                out=factor_codes[:, g].bitcast(FP8X4),
-                scales=factor_scales[:, g],
-                in_=factor_woven[g][:].rearrange("p m t -> p (m t)"),
+                out=factor_codes[:, g, lo:hi].bitcast(FP8X4),
+                scales=factor_scales[:, g, lo:hi],
+                in_=factor_woven[g][:, lo:hi, :].rearrange("p m t -> p (m t)"),
             )
 
         def turn_basis(pool, n):
@@ -178,9 +185,9 @@ def tile_promp_trajectory_sampling_s7_kernel(
             if c not in noise_planes:
                 noise_planes[c] = stage.tile([P, PACK, WIDTHS[c]], BF16, name="noise_planes", bufs=4)
             hi = hi or WIDTHS[c]
-            bytes_in, base = noise_in[STARTS[c] + lo]
             for t in range(first, end):
-                src = bytes_in[:, t, STARTS[c] + lo - base : STARTS[c] + hi - base].bitcast(FP8)
+                bytes_in, base = noise_in[STARTS[c] + lo, t]
+                src = bytes_in[:, STARTS[c] + lo - base : STARTS[c] + hi - base].bitcast(FP8)
                 dst = noise_planes[c][:, t, lo:hi]
                 scale = byte_scale[:, t : t + 1]
                 if engine == "scalar":
@@ -343,35 +350,39 @@ def tile_promp_trajectory_sampling_s7_kernel(
                 finish_tile(ahead[c, n], c, n)
 
         with tc.manual_schedule():
-            load_noise(0, 768)
+            load_noise(0, 768, 0, 2)
+            load_noise(0, 768, 2, 4)
             nc.scalar.dma_start(out=byte_scale[:], in_=noise_scale.rearrange("(p t) o -> p (t o)", t=PACK))
+            nc.scalar.dma_start(out=amp_in[:], in_=amp[: N // 2].rearrange("(q e) -> q e", e=8))
             load_factor(0, 0)
             load_factor(0, 1)
             load_factor(1, 0)
             load_factor(1, 1)
-            nc.scalar.dma_start(out=mean_cols[:], in_=mean.rearrange("(g p t) -> p g t", g=PASSES, t=PACK))
-            load_noise(768, 2048)
+            load_noise(768, 1280)
+            nc.sync.dma_start(out=mean_cols[:], in_=mean.rearrange("(g p t) -> p g t", g=PASSES, t=PACK))
+            load_noise(1280, 2048)
             load_basis(0, 2)
             load_basis(2, 4)
             load_basis(4, 6)
             load_basis(6, 8)
-            load_amp(0, 2)
             nc.sync.dma_start(out=rnorm_cols[:], in_=rnorm.rearrange("(p n) -> p n", n=TILES))
-            load_amp(2, 5)
+            nc.sync.dma_start(out=amp_all[:, N // 2 :], in_=amp[N // 2 :].partition_broadcast(P))
             make_identity(nc, identity[:])
             table_in = keep.tile([P, 1], F32, name="table_in")
             nc.vector.memset(table_in[:], 0.0)
             nc.scalar.activation(out=table_in[:], in_=table_in[:], func=IDENTITY)
 
-            widen_noise("vector", 0)
+            widen_noise("vector", 0, 0, 2)
+            widen_noise("vector", 1, 0, 1, 0, HALF)
+            widen_noise("vector", 0, 2, 4)
+            widen_noise("vector", 1, 0, 1, HALF, BANK)
             noise_woven[0] = woven_tile("woven_v", 5)
-            widen_noise("vector", 1, 0, 1)
             weave_noise("vector", 0, 0, HALF)
             widen_noise("scalar", 1, 1, 4)
-            quantize_noise(0)
             noise_woven[1] = woven_tile("woven_v", 5)
             factor_woven[0] = woven_tile("woven_v", 5)
             factor_woven[1] = woven_tile("ring_a", 1)
+            spread_amp()
             turned = {}
             for g in range(PASSES):
                 for a in range(2):
@@ -380,9 +391,11 @@ def tile_promp_trajectory_sampling_s7_kernel(
                 for a in range(2):
                     empty_factor(nc.scalar.copy, turned[g, a], g, a)
             weave_noise("vector", 1, 0, BANK)
+            quantize_noise(0)
             quantize_factor(0)
             quantize_noise(1)
-            quantize_factor(1)
+            quantize_factor(1, 0, HALF)
+            quantize_factor(1, HALF, BANK)
             w_woven[0] = woven_tile("woven_v", 5)
             w_woven[1] = woven_tile("woven_v", 5)
             w_woven[2] = woven_tile("ring_c", 1)

from contextlib import ExitStack

import concourse.mybir as mybir
from concourse.masks import make_identity

T, B, R, N = 1024, 1024, 512, 2048
FLOPS = 2 * B * R * N + 2 * T * B * N

F32 = mybir.dt.float32
BF16 = mybir.dt.bfloat16
U32 = mybir.dt.uint32
U8 = mybir.dt.uint8
FP8 = mybir.dt.float8_e4m3fn
FP8X4 = mybir.dt.float8_e4m3fn_x4
ADD = mybir.AluOpType.add
MULT = mybir.AluOpType.mult
COPY = mybir.ActivationFunctionType.Copy
IDENTITY = mybir.ActivationFunctionType.Identity

P = 128
PACK = 4
PASSES = B // (P * PACK)
BANK = 512
HALF = BANK // 2
TILES = T // P
WIDTHS = (HALF, BANK, BANK, BANK, HALF)
STARTS = tuple(sum(WIDTHS[:c]) for c in range(len(WIDTHS)))
CHUNKS = len(WIDTHS)


def piece_of(c, g):
    if c == 0:
        return 0, HALF * g
    if c == CHUNKS - 1:
        return 2 * c - 1, HALF * g
    return 2 * c - 1 + g, 0


def source_of(u, col):
    c = (u + 1) // 2
    if WIDTHS[c] == HALF:
        return col // HALF, STARTS[c] + col % HALF
    return (u - 1) % 2, STARTS[c] + col


def tile_promp_trajectory_sampling_s7_kernel(
    tc, factor, noise_bytes, noise_scale, mean, basis, rnorm, amp, out
):
    nc = tc.nc
    with ExitStack() as ctx:
        keep = ctx.enter_context(tc.tile_pool(name="keep", bufs=1))
        stage = ctx.enter_context(tc.tile_pool(name="stage", bufs=2))
        psum_a = ctx.enter_context(tc.psum_pool(name="psum_a", bufs=8))
        psum_b = psum_a

        factor_woven = {}
        factor_codes = keep.tile([P, PASSES, PACK * P], U32, name="factor_codes", align_bytes=256)
        factor_scales = keep.tile([P, PASSES, PACK * P], U8, name="factor_scales", align_bytes=256)
        basis_woven = {}
        basis_codes = keep.tile([P, TILES, PASSES * P], U32, name="basis_codes", align_bytes=256)
        basis_scales = keep.tile([P, TILES, PASSES * P], U8, name="basis_scales", align_bytes=256)
        noise_codes = keep.tile([P, N], U32, name="noise_codes", align_bytes=256)
        noise_scales = keep.tile([P, N], U8, name="noise_scales", align_bytes=256)
        byte_scale = keep.tile([P, PACK], F32, name="byte_scale")
        mean_cols = keep.tile([P, PASSES, PACK], BF16, name="mean_cols")
        rnorm_cols = keep.tile([P, TILES], BF16, name="rnorm_cols")
        identity = keep.tile([P, P], F32, name="identity")

        factor_hbm = factor.rearrange("(g m t) r -> g m t r", g=PASSES, t=PACK)
        noise_hbm = noise_bytes.rearrange("(p t) j -> p t j", t=PACK)
        basis_hbm = basis.rearrange("(p n) b -> p n b", n=TILES)
        out_hbm = out.rearrange("(p n) j -> p n j", n=TILES)

        factor_rows = {}
        basis_rows = {}
        noise_in = {}
        amp_rows = {}

        def columns(c):
            return slice(STARTS[c], STARTS[c] + WIDTHS[c])

        def load_factor(g, a):
            factor_rows[g, a] = keep.tile([P, 2, R], BF16, name=f"factor_rows_{g}_{a}", align_bytes=256)
            nc.sync.dma_start(out=factor_rows[g, a][:], in_=factor_hbm[g][:, 2 * a : 2 * a + 2, :])

        def load_noise(lo, hi, first=0, end=PACK):
            bytes_in = keep.tile([P, end - first, hi - lo], U8, name=f"noise_in_{lo}_{first}", align_bytes=256)
            nc.sync.dma_start(out=bytes_in[:], in_=noise_hbm[:, first:end, lo:hi])
            for j in range(lo, hi, HALF):
                for t in range(first, end):
                    noise_in[j, t] = (bytes_in[:, t - first, :], lo)

        def load_basis(first, end):
            rows = keep.tile([P, end - first, B], BF16, name=f"basis_rows_{first}", align_bytes=256)
            nc.sync.dma_start(out=rows[:], in_=basis_hbm[:, first:end, :])
            for n in range(first, end):
                basis_rows[n] = rows[:, n - first, :]

        amp_in = keep.tile([P, 8], BF16, name="amp_in")
        amp_all = keep.tile([P, N], BF16, name="amp_all", align_bytes=256)
        for c in range(CHUNKS):
            amp_rows[c] = amp_all[:, columns(c)]

        def spread_amp():
            bank = psum_a.tile([P, 4, P], F32, name="bank")
            words = amp_in[:].bitcast(F32)
            for m in range(4):
                nc.tensor.transpose(bank[:, m, :], words[:, m : m + 1].to_broadcast([P, P]), identity[:])
            words = amp_all[:, : N // 2].bitcast(F32)
            nc.scalar.copy(out=words.rearrange("p (q m) -> p q m", m=4), in_=bank[:].rearrange("p m q -> p q m"))

        def turn_factor(pool, g, a):
            bank = pool.tile([P, 2, 2, P], F32, name="bank")
            words = factor_rows[g, a][:].bitcast(F32)
            for x in range(2):
                for u in range(2):
                    nc.tensor.transpose(bank[:, x, u, :], words[:, x, u::2], identity[:])
            return bank

        def empty_factor(copy, bank, g, a):
            woven = factor_woven[g][:, HALF * a : HALF * (a + 1), :].rearrange("p m t -> p (m t)").bitcast(F32)
            copy(
                out=woven.rearrange("p (x m u) -> p x m u", x=2, u=2),
                in_=bank[:].rearrange("p x u m -> p x m u"),
            )

        def quantize_factor(g, lo=0, hi=BANK):
            nc.vector.quantize_mx(
                out=factor_codes[:, g, lo:hi].bitcast(FP8X4),
                scales=factor_scales[:, g, lo:hi],
                in_=factor_woven[g][:, lo:hi, :].rearrange("p m t -> p (m t)"),
            )

        def turn_basis(pool, n):
            bank = pool.tile([P, PASSES, 2, P], F32, name="bank")
            words = basis_rows[n].bitcast(F32)
            for g in range(PASSES):
                first = P * 2 * g
                for u in range(2):
                    nc.tensor.transpose(bank[:, g, u, :], words[:, first + u : first + P * 2 : 2], identity[:])
            return bank

        def empty_basis(copy, bank, n):
            if n % 4 == 0:
                basis_woven[n // 4] = stage.tile(
                    [P, 4, PASSES, P, PACK], BF16, name=f"basis_woven_{n // 4}", align_bytes=256, bufs=1
                )
            woven = basis_woven[n // 4][:, n % 4].rearrange("p g m t -> p (g m t)").bitcast(F32)
            copy(
                out=woven.rearrange("p (g m u) -> p g m u", g=PASSES, u=2),
                in_=bank[:].rearrange("p g u m -> p g m u"),
            )

        def quantize_basis(first, end):
            some = slice(first, end)
            nc.vector.quantize_mx(
                out=basis_codes[:, some].rearrange("p n k -> p (n k)").bitcast(FP8X4),
                scales=basis_scales[:, some].rearrange("p n k -> p (n k)"),
                in_=basis_woven[first // 4][:].rearrange("p n g m t -> p (n g m t)"),
            )

        def weave(engine, woven, planes, first, end):
            dst = woven[:, first:end, :]
            src = planes[:, :, first:end]
            if engine == "gpsimd":
                nc.gpsimd.tensor_scalar(
                    out=dst.rearrange("p (j i) t -> p j t i", i=4),
                    in0=src.rearrange("p t (j i) -> p j t i", i=4),
                    scalar1=1.0,
                    scalar2=0.0,
                    op0=MULT,
                    op1=ADD,
                )
                return
            copy = nc.scalar.copy if engine == "scalar" else nc.vector.tensor_copy
            copy(
                out=dst.rearrange("p (j i) t -> p j t i", i=4),
                in_=src.rearrange("p t (j i) -> p j t i", i=4),
            )

        noise_planes = {}
        noise_woven = {}

        def widen_noise(engine, c, first=0, end=PACK, lo=0, hi=None):
            if c not in noise_planes:
                noise_planes[c] = stage.tile([P, PACK, WIDTHS[c]], BF16, name="noise_planes", bufs=4)
            hi = hi or WIDTHS[c]
            for t in range(first, end):
                bytes_in, base = noise_in[STARTS[c] + lo, t]
                src = bytes_in[:, STARTS[c] + lo - base : STARTS[c] + hi - base].bitcast(FP8)
                dst = noise_planes[c][:, t, lo:hi]
                scale = byte_scale[:, t : t + 1]
                if engine == "scalar":
                    nc.scalar.activation(out=dst, in_=src, func=COPY, scale=scale)
                else:
                    nc.vector.tensor_scalar(out=dst, in0=src, scalar1=scale, scalar2=None, op0=MULT)

        def woven_tile(tag, bufs):
            return stage.tile([P, BANK, PACK], BF16, name=tag, align_bytes=256, bufs=bufs)

        def weave_noise(engine, c, first, end):
            weave(engine, noise_woven[c], noise_planes[c], first, end)

        def quantize_noise(c):
            nc.vector.quantize_mx(
                out=noise_codes[:, columns(c)].bitcast(FP8X4),
                scales=noise_scales[:, columns(c)],
                in_=noise_woven[c][:, : WIDTHS[c], :].rearrange("p j t -> p (j t)"),
            )

        w_planes = {}
        w_woven = {}
        w_codes = {}
        w_scales = {}

        def first_pass(dst, g, t, j, width):
            rows = slice(P * t, P * (t + 1))
            nc.tensor.matmul_mx(
                out=dst,
                lhsT=factor_codes[:, g, rows].bitcast(FP8X4),
                lhsT_scale=factor_scales[:, g, rows],
                rhs=noise_codes[:, j : j + width].bitcast(FP8X4),
                rhs_scale=noise_scales[:, j : j + width],
                start=True,
                stop=True,
            )

        def first_quarter(pool, u, quarter):
            g, j = source_of(u, P * quarter)
            bank = pool.tile([P, PACK, P], F32, name="bank")
            for t in range(PACK):
                first_pass(bank[:, t, :], g, t, j, P)
            return bank

        def empty_quarter(bank, u, quarter):
            g, j = source_of(u, P * quarter)
            nc.vector.tensor_tensor(
                out=w_woven[u][:, P * quarter : P * (quarter + 1), :],
                in0=bank[:].rearrange("p t j -> p j t"),
                in1=mean_cols[:, g, :].unsqueeze(1).to_broadcast([P, P, PACK]),
                op=ADD,
            )

        def first_bank(pool, u, x):
            if x == 0:
                w_planes[u] = stage.tile([P, PACK, BANK], BF16, name="w_planes", bufs=3)
            bank = pool.tile([P, BANK], F32, name="bank")
            if WIDTHS[(u + 1) // 2] == BANK:
                g, j = source_of(u, 0)
                parts = [(g, x, j, 0, 0, BANK)]
            else:
                g, j = source_of(u, HALF * (x // 2))
                parts = [(g, 2 * (x % 2) + y, j, HALF * y, HALF * g, HALF) for y in range(2)]
            for g, t, j, at, to, width in parts:
                first_pass(bank[:, at : at + width], g, t, j, width)
            for g, t, j, at, to, width in parts:
                nc.scalar.activation(
                    out=w_planes[u][:, t, to : to + width],
                    in_=bank[:, at : at + width],
                    func=IDENTITY,
                    bias=mean_cols[:, g, t : t + 1],
                )

        def weave_w(engine, u, first, end):
            weave(engine, w_woven[u], w_planes[u], first, end)

        def quantize_w(u):
            w_codes[u] = keep.tile([P, BANK], U32, name=f"w_codes_{u}", align_bytes=256)
            w_scales[u] = keep.tile([P, BANK], U8, name=f"w_scales_{u}", align_bytes=256)
            nc.vector.quantize_mx(
                out=w_codes[u][:].bitcast(FP8X4),
                scales=w_scales[u][:],
                in_=w_woven[u][:].rearrange("p j t -> p (j t)"),
            )

        results = {}

        def second_pass(bank, c, n, g):
            u, at = piece_of(c, g)
            phases = slice(P * g, P * (g + 1))
            nc.tensor.matmul_mx(
                out=bank,
                lhsT=basis_codes[:, n, phases].bitcast(FP8X4),
                lhsT_scale=basis_scales[:, n, phases],
                rhs=w_codes[u][:, at : at + WIDTHS[c]].bitcast(FP8X4),
                rhs_scale=w_scales[u][:, at : at + WIDTHS[c]],
                start=(g == 0),
                stop=(g == PASSES - 1),
            )

        def finish_tile(bank, c, n):
            group = 2 * BANK // WIDTHS[c]
            if c == CHUNKS - 1 and n >= TILES - group:
                group = group // 2
            first = n - n % group
            if n == first:
                results[c, first] = stage.tile([P, group, WIDTHS[c]], F32, name="result", bufs=16, align_bytes=256)
            result = results[c, first]
            nc.vector.scalar_tensor_tensor(
                out=result[:, n - first, :],
                in0=bank,
                scalar=rnorm_cols[:, n : n + 1],
                in1=amp_rows[c],
                op0=MULT,
                op1=MULT,
            )
            if n == first + group - 1:
                queue = nc.scalar if (c, first) in ((3, 2), (3, 6), (4, 4)) else nc.sync
                queue.dma_start(out=out_hbm[:, first : first + group, columns(c)], in_=result[:])

        def basis_tiles(first, end):
            banks = [turn_basis(psum_a, n) for n in range(first, end)]
            for n in range(first, end):
                empty_basis(nc.scalar.copy, banks[n - first], n)

        def fused(u, q):
            empty_quarter(first_quarter(psum_b, u, q), u, q)

        def piece(u, first=0, end=4):
            for x in range(first, end):
                first_bank(psum_a, u, x)

        def tiles(c, first, end):
            step = BANK // WIDTHS[c]
            for n in range(first, end, step):
                multiply(c, n, n + step)
                finish(c, n, n + step)

        ahead = {}

        def multiply(c, first, end):
            for n in range(first, end):
                if WIDTHS[c] == BANK:
                    ahead[c, n] = psum_b.tile([P, BANK], F32, name="bank")[:]
                elif n % 2 == 0:
                    both = psum_b.tile([P, 2, HALF], F32, name="bank")
                    ahead[c, n], ahead[c, n + 1] = both[:, 0, :], both[:, 1, :]
                for g in range(PASSES):
                    second_pass(ahead[c, n], c, n, g)

        def multiply_by_pass(c, first, end):
            for n in range(first, end):
                ahead[c, n] = psum_b.tile([P, BANK], F32, name="bank")[:]
                second_pass(ahead[c, n], c, n, 0)
            for n in range(first, end):
                second_pass(ahead[c, n], c, n, 1)

        def finish(c, first, end):
            for n in range(first, end):
                finish_tile(ahead[c, n], c, n)

        with tc.manual_schedule():
            load_noise(0, 768, 0, 2)
            load_noise(0, 768, 2, 4)
            nc.scalar.dma_start(out=byte_scale[:], in_=noise_scale.rearrange("(p t) o -> p (t o)", t=PACK))
            nc.scalar.dma_start(out=amp_in[:], in_=amp[: N // 2].rearrange("(q e) -> q e", e=8))
            load_factor(0, 0)
            load_factor(0, 1)
            load_factor(1, 0)
            load_factor(1, 1)
            load_noise(768, 1280)
            nc.sync.dma_start(out=mean_cols[:], in_=mean.rearrange("(g p t) -> p g t", g=PASSES, t=PACK))
            load_noise(1280, 2048)
            load_basis(0, 2)
            load_basis(2, 4)
            load_basis(4, 6)
            load_basis(6, 8)
            nc.sync.dma_start(out=rnorm_cols[:], in_=rnorm.rearrange("(p n) -> p n", n=TILES))
            nc.sync.dma_start(out=amp_all[:, N // 2 :], in_=amp[N // 2 :].partition_broadcast(P))
            make_identity(nc, identity[:])
            table_in = keep.tile([P, 1], F32, name="table_in")
            nc.vector.memset(table_in[:], 0.0)
            nc.scalar.activation(out=table_in[:], in_=table_in[:], func=IDENTITY)

            widen_noise("vector", 0, 0, 2)
            widen_noise("vector", 1, 0, 1, 0, HALF)
            widen_noise("vector", 0, 2, 4)
            widen_noise("vector", 1, 0, 1, HALF, BANK)
            noise_woven[0] = woven_tile("woven_v", 5)
            weave_noise("vector", 0, 0, HALF)
            widen_noise("scalar", 1, 1, 4)
            noise_woven[1] = woven_tile("woven_v", 5)
            factor_woven[0] = woven_tile("woven_v", 5)
            factor_woven[1] = woven_tile("ring_a", 1)
            spread_amp()
            turned = {}
            for g in range(PASSES):
                for a in range(2):
                    turned[g, a] = turn_factor(psum_a, g, a)
            for g in range(PASSES):
                for a in range(2):
                    empty_factor(nc.scalar.copy, turned[g, a], g, a)
            weave_noise("vector", 1, 0, BANK)
            quantize_noise(0)
            quantize_factor(0)
            quantize_noise(1)
            quantize_factor(1, 0, HALF)
            quantize_factor(1, HALF, BANK)
            w_woven[0] = woven_tile("woven_v", 5)
            w_woven[1] = woven_tile("woven_v", 5)
            w_woven[2] = woven_tile("ring_c", 1)
            noise_woven[2] = woven_tile("ring_a", 1)
            for lo in (0, HALF):
                widen_noise("scalar", 2, 0, 4, lo, lo + HALF)
                weave_noise("gpsimd", 2, lo, lo + HALF)
            widen_noise("scalar", 3)
            fused(0, 0)
            fused(0, 1)
            fused(1, 0)
            fused(1, 1)
            fused(1, 2)
            fused(1, 3)
            fused(0, 2)
            quantize_noise(2)
            noise_woven[3] = woven_tile("ring_a", 1)
            weave_noise("gpsimd", 3, 0, 3 * P)
            fused(0, 3)
            basis_tiles(0, 2)
            fused(2, 0)
            fused(2, 1)
            weave_noise("scalar", 3, 3 * P, BANK)
            basis_tiles(2, 4)
            fused(2, 2)
            fused(2, 3)
            piece(3, 0, 2)
            basis_tiles(4, 6)
            piece(3, 2, 4)
            basis_tiles(6, 8)
            quantize_w(0)
            quantize_basis(0, 4)
            multiply(0, 0, 4)
            widen_noise("scalar", 4)
            quantize_w(1)
            quantize_w(2)
            quantize_noise(3)
            finish(0, 0, 4)
            piece(4, 0, 2)
            multiply(1, 0, 2)
            piece(4, 2, 4)
            multiply(1, 2, 4)
            quantize_basis(4, 8)
            w_woven[3] = woven_tile("basis_woven_1", 1)
            weave_w("gpsimd", 3, 0, BANK)
            noise_woven[4] = woven_tile("ring_b", 1)
            weave_noise("gpsimd", 4, 0, HALF)
            w_woven[4] = woven_tile("ring_c", 1)
            weave_w("scalar", 4, 0, BANK)
            finish(1, 0, 2)
            multiply(0, 4, 8)
            finish(1, 2, 4)
            piece(5, 0, 2)
            multiply(1, 4, 6)
            finish(0, 4, 8)
            piece(5, 2, 4)
            multiply(1, 6, 8)
            finish(1, 4, 6)
            piece(6, 0, 2)
            quantize_noise(4)
            quantize_w(3)
            quantize_w(4)
            w_woven[5] = woven_tile("ring_c", 1)
            weave_w("gpsimd", 5, 0, BANK)
            multiply_by_pass(2, 0, 2)
            piece(6, 2, 4)
            w_woven[6] = woven_tile("ring_b", 1)
            weave_w("gpsimd", 6, 0, P)
            weave_w("scalar", 6, P, BANK)
            finish(1, 6, 8)
            finish(2, 0, 2)
            tiles(2, 2, 6)
            multiply(2, 6, 8)
            piece(7)
            quantize_w(5)
            quantize_w(6)
            w_woven[7] = woven_tile("ring_b", 1)
            weave_w("gpsimd", 7, 0, HALF)
            weave_w("scalar", 7, HALF, BANK)
            multiply_by_pass(3, 0, 2)
            finish(2, 6, 8)
            finish(3, 0, 2)
            tiles(3, 2, 5)
            multiply(3, 5, 8)
            quantize_w(7)
            finish(3, 5, 8)
            tiles(4, 0, 8)
